import numpy as np
import ml_dtypes


def mxq(x, axis, fmt="e4m3"):
    dtype, down = {"e4m3": (ml_dtypes.float8_e4m3fn, 7), "e5m2": (ml_dtypes.float8_e5m2, 14)}[fmt]
    v = np.moveaxis(np.asarray(x, np.float32).astype(ml_dtypes.bfloat16).astype(np.float64), axis, -1)
    blocks = v.reshape(v.shape[:-1] + (-1, 32))
    amax = np.abs(blocks).max(-1, keepdims=True)
    byte = np.maximum(np.where(amax > 0, np.frexp(amax)[1] - 1 + 127, 0) - down, 1)
    scale = np.exp2(byte - 127.0)
    codes = (blocks / scale).astype(np.float32).astype(dtype).astype(np.float64)
    return np.moveaxis((codes * scale).reshape(v.shape), -1, axis)


WIDE = False


def mx_kscale(k):
    if not WIDE:
        return np.ones(k)
    levels = np.array([10, -10, 5, -5, 0])
    if k % 512:
        return np.exp2(np.random.permutation(np.resize(levels, k // 32))).repeat(32)
    a = np.empty((k // 512, 16))
    for p in range(k // 512):
        a[p, :8] = np.random.permutation(np.resize(levels, 8))
        for g in range(8):
            far = levels[np.abs(levels - a[p, g]) >= 10]
            a[p, g + 8] = far[np.random.randint(len(far))]
    return np.exp2(a.ravel()).repeat(32)


def f64(x):
    return np.asarray(x).astype(np.float64)


def striped(idx):
    return np.tile(idx.reshape(-1, 16).T, (8, 1)).astype(np.uint16)


def unstriped(offs):
    return offs[:16].T.reshape(-1).astype(np.int64)


E2M1 = np.array([0.0, 0.5, 1.0, 1.5, 2.0, 3.0, 4.0, 6.0, -0.0, -0.5, -1.0, -1.5, -2.0, -3.0, -4.0, -6.0])


def pack_weight(w, fmt):
    k, n = w.shape
    w = f64(np.asarray(w, np.float32).astype(ml_dtypes.bfloat16)).reshape(k // 32, 32, n)
    amax = np.abs(w).max(1)
    if fmt == "e4m3":
        byte = np.frexp(amax)[1] - 1 + 127 - 7
    else:
        mant, ex = np.frexp(amax / 6.0)
        byte = np.where(mant > 0.5, ex, ex - 1) + 127
    byte = np.clip(np.where(amax > 0, byte, 1), 1, 254)
    scaled = (w * np.exp2(127.0 - byte)[:, None, :]).reshape(k, n).astype(np.float32)
    by_word = np.ascontiguousarray(scaled.reshape(k // 512, 128, 4, n).transpose(0, 1, 3, 2))
    if fmt == "e4m3":
        words = by_word.astype(ml_dtypes.float8_e4m3fn).view(np.uint8)
    else:
        c = by_word.astype(ml_dtypes.float4_e2m1fn).view(np.uint8) & 0xF
        words = (c[..., 0::2] | (c[..., 1::2] << 4)).reshape(k // 512, 128, 2 * n)
    return np.ascontiguousarray(words), np.ascontiguousarray(byte.astype(np.uint8).reshape(k // 512, 16, n))


def unpack_weight(words, scales, fmt):
    g, _, n = scales.shape
    words = np.ascontiguousarray(words).reshape(g, 128, n, -1)
    if fmt == "e4m3":
        vals = words.view(ml_dtypes.float8_e4m3fn).astype(np.float64)
    else:
        nib = np.empty((g, 128, n, 4), np.uint8)
        nib[..., 0::2] = words & 0xF
        nib[..., 1::2] = words >> 4
        vals = E2M1[nib]
    vals = vals * np.repeat(np.exp2(scales.astype(np.float64) - 127.0), 8, axis=1)[..., None]
    return vals.transpose(0, 1, 3, 2).reshape(g * 512, n)


def gelu(v):
    return 0.5 * v * (1.0 + np.tanh(np.sqrt(2.0 / np.pi) * (v + 0.044715 * v**3)))


def striped8(idx):
    return np.concatenate([v.reshape(-1, 16).T for v in idx]).astype(np.uint16)


def unstriped8(offs):
    return np.stack([offs[16 * g:16 * g + 16].T.reshape(-1) for g in range(8)]).astype(np.int64)


def heads(xT, wgt, idx8):
    k = np.arange(xT.shape[0])
    return wgt[k // 4 % 128] * xT[k[:, None], idx8[k % 512 // 64]]


KX, T, KG, TG, S, H, N, G, R = 1024, 2048, 512, 1024, 512, 1024, 256, 8, 16

def setup_inputs():
    n = np.random.standard_normal
    s, sg, u = mx_kscale(KX)[:, None], mx_kscale(KG)[:, None], mx_kscale(H)[:, None]
    tab_words, tab_scales = pack_weight(n((KG, TG)) * sg, "e4m3")
    wg_words, wg_scales = pack_weight(n((KG, H)) / np.sqrt(KG) / sg * u.T, "e2m1")
    wv_words, wv_scales = pack_weight(n((H, N)) / np.sqrt(H) / u, "e4m3")
    return {
        "xT": (n((KX, T)) * s).astype(np.float32),
        "wgt": np.repeat(np.random.uniform(0.5, 2.0, (G, S)), R, axis=0).astype(np.float32),
        "offs2": striped8(np.stack([np.random.permutation(T)[:S] for _ in range(G)])),
        "tab_words": tab_words, "tab_scales": tab_scales,
        "offs": striped(np.random.permutation(TG)[:S]),
        "wa": (n((KX, H)) / np.sqrt(KX) / s * u.T).astype(np.float32),
        "wb": (n((KX, H)) / np.sqrt(KX) / s).astype(np.float32),
        "bb": (0.5 * n(H)).astype(np.float32),
        "wg_words": wg_words, "wg_scales": wg_scales,
        "wv_words": wv_words, "wv_scales": wv_scales,
        "bv": (0.5 * n(N)).astype(np.float32),
    }

def reference(xT, wgt, offs2, tab_words, tab_scales, offs, wa, wb, bb, wg_words, wg_scales, wv_words, wv_scales, bv):
    xg = mxq(heads(f64(xT), f64(wgt), unstriped8(offs2)), 0, "e4m3")
    v = unpack_weight(tab_words, tab_scales, "e4m3")[:, unstriped(offs)]
    wg = unpack_weight(wg_words, wg_scales, "e2m1")
    wv = unpack_weight(wv_words, wv_scales, "e4m3")
    a = mxq(f64(wa), 0, "e4m3").T @ xg
    b = (mxq(f64(wb), 0, "e4m3").T @ xg) + f64(bb)[:, None]
    g = wg.T @ v
    h = a * (1.0 / (1.0 + np.exp(-b))) + g
    return (wv.T @ mxq(h, 0, "e4m3")) + f64(bv)[:, None]

@@ -1,0 +1,272 @@
+from contextlib import ExitStack
+
+import concourse.mybir as mybir
+
+KX, T, KG, TG, S, H, N = 1024, 2048, 512, 1024, 512, 1024, 256
+FLOPS = 2 * S * (2 * KX * H + KG * H + H * N)
+
+F32 = mybir.dt.float32
+BF16 = mybir.dt.bfloat16
+I32 = mybir.dt.int32
+U32 = mybir.dt.uint32
+U16 = mybir.dt.uint16
+U8 = mybir.dt.uint8
+FP8X4 = mybir.dt.float8_e4m3fn_x4
+FP4X4 = mybir.dt.float4_e2m1fn_x4
+MULT = mybir.AluOpType.mult
+ADD = mybir.AluOpType.add
+SIGMOID = mybir.ActivationFunctionType.Sigmoid
+IDENTITY = mybir.ActivationFunctionType.Identity
+
+P = 128
+PACK = 4
+KP = P * PACK
+ALIGN = 64
+TAIL = 128
+
+
+def tile_list_replay_goal_value_kernel(
+    tc, xT, wgt, offs2, tab_words, tab_scales, offs, wa, wb, bb, wg_words, wg_scales, wv_words, wv_scales, bv, out
+):
+    nc = tc.nc
+
+    def cast_copy(engine, dst, src):
+        if engine == "S":
+            nc.scalar.copy(dst, src)
+        else:
+            nc.vector.tensor_copy(dst, src)
+
+    with ExitStack() as ctx:
+        keep = ctx.enter_context(tc.tile_pool(name="keep", bufs=1))
+        big = ctx.enter_context(tc.tile_pool(name="big", bufs=10))
+        stage = ctx.enter_context(tc.tile_pool(name="stage", bufs=2))
+        halves = ctx.enter_context(tc.tile_pool(name="halves", bufs=6))
+        psum = ctx.enter_context(tc.psum_pool(name="psum", bufs=1))
+
+        def bank(n, shape):
+            return psum.tile(shape, F32, name="bank%d" % n)
+
+        goal_list = keep.tile([P, S // 16], U16, name="goal_list")
+        head_lists = keep.tile([P, S // 16], U16, name="head_lists")
+        tab_w = keep.tile([P, TG], U32, name="tab_w", align_bytes=ALIGN)
+        tab_s = keep.tile([P, TG], U8, name="tab_s", align_bytes=ALIGN)
+        wg_raw_w = keep.tile([P, 2 * H], U8, name="wg_raw_w", align_bytes=ALIGN)
+        wg_raw_s = keep.tile([P, H], U8, name="wg_raw_s", align_bytes=ALIGN)
+        wv_w = keep.tile([P, 2, N], U32, name="wv_w", align_bytes=ALIGN)
+        wv_s = keep.tile([P, 2, N], U8, name="wv_s", align_bytes=ALIGN)
+        wgt_sb = keep.tile([P, S], F32, name="wgt_sb")
+        bb_sb = keep.tile([P, 2, PACK], F32, name="bb_sb")
+        bv_sb = keep.tile([P, 2], F32, name="bv_sb")
+        warm = keep.tile([P, 2], F32, name="warm")
+
+        nc.vector.memset(tab_s[:].bitcast(I32), 0)
+        nc.vector.memset(wg_raw_s[:].bitcast(I32), 0)
+        nc.vector.memset(wv_s[:].rearrange("p a e -> p (a e)").bitcast(I32), 0)
+        nc.vector.memset(warm[:, 0:1], 0.0)
+        nc.scalar.activation(warm[:, 1:2], warm[:, 0:1], SIGMOID)
+
+        def load_x(a, i):
+            plane = big.tile([P, T], F32, name="big")
+            rows = xT[a * KP : (a + 1) * KP, :].rearrange("(p i) t -> p i t", i=PACK)
+            nc.sync.dma_start(plane[:], rows[:, i, :])
+            return plane
+
+        def load_w(w, b, a):
+            raw = big.tile([P, PACK, KP], F32, name="big")
+            src = w[a * KP : (a + 1) * KP, b * KP : (b + 1) * KP]
+            nc.sync.dma_start(raw[:], src.rearrange("(p j) c -> p j c", j=PACK))
+            return raw
+
+        nc.sync.dma_start(goal_list[:], offs)
+        nc.sync.dma_start(tab_w[:].bitcast(I32), tab_words[0].rearrange("p t i -> p (t i)").bitcast(I32))
+        for q in range(4):
+            nc.sync.dma_start(tab_s[32 * q : 32 * q + 4, :].bitcast(I32), tab_scales[0, 4 * q : 4 * q + 4, :].bitcast(I32))
+        nc.sync.dma_start(wg_raw_w[:].bitcast(I32), wg_words[0].bitcast(I32))
+        x_planes = {(0, 0): load_x(0, 0)}
+        for q in range(4):
+            nc.sync.dma_start(wg_raw_s[32 * q : 32 * q + 4, :].bitcast(I32), wg_scales[0, 4 * q : 4 * q + 4, :].bitcast(I32))
+        nc.sync.dma_start(head_lists[:], offs2)
+        nc.sync.dma_start(wgt_sb[:], wgt)
+        for n in range(1, 8):
+            x_planes[(n // 4, n % 4)] = load_x(n // 4, n % 4)
+            if n == 2:
+                nc.sync.dma_start(bb_sb[:], bb.rearrange("(b p t) -> p b t", p=P, t=PACK))
+                with nc.allow_non_contiguous_dma(reason="one bias value for each partition and half"):
+                    nc.sync.dma_start(bv_sb[:], bv.rearrange("(h p) -> p h", p=P))
+            if n == 4:
+                for q in range(4):
+                    nc.sync.dma_start(
+                        wv_s[32 * q : 32 * q + 4, :, :].bitcast(I32),
+                        wv_scales[:, 4 * q : 4 * q + 4, :].rearrange("a q e -> q a e").bitcast(I32),
+                    )
+        raw_w = {}
+        for b in range(2):
+            for name, w in (("b", wb), ("a", wa)):
+                for a in range(2):
+                    raw_w[(name, b, a)] = load_w(w, b, a)
+        nc.sync.dma_start(wv_w[:].bitcast(I32), wv_words.rearrange("a p e i -> p a (e i)").bitcast(I32))
+
+        v_w = keep.tile([P, S], U32, name="v_w", align_bytes=ALIGN)
+        v_s = keep.tile([P, S], U8, name="v_s", align_bytes=ALIGN)
+        nc.vector.tensor_copy(v_w[:], tab_w[:].indirect(goal_list[:]))
+        nc.vector.tensor_copy(v_s[:], tab_s[:].indirect(goal_list[:]))
+        wg_w = keep.tile([P, 2 * H], U8, name="wg_w", align_bytes=ALIGN)
+        wg_s = keep.tile([P, H], U8, name="wg_s", align_bytes=ALIGN)
+        nc.vector.tensor_copy(
+            wg_w[:].bitcast(U16).rearrange("p (b t m) -> p b m t", b=2, t=PACK),
+            wg_raw_w[:].bitcast(U16).rearrange("p (b m t) -> p b m t", b=2, t=PACK),
+        )
+        nc.vector.tensor_copy(
+            wg_s[:].rearrange("p (b t m) -> p b m t", b=2, t=PACK),
+            wg_raw_s[:].rearrange("p (b m t) -> p b m t", b=2, t=PACK),
+        )
+        goal = [keep.tile([P, PACK, S], F32, name="goal%d" % b) for b in range(2)]
+        for b in range(2):
+            for t in range(PACK):
+                n = PACK * b + t
+                acc = bank(n, [P, S])
+                nc.tensor.matmul_mx(
+                    out=acc[:],
+                    lhsT=wg_w[:, 2 * P * n : 2 * P * (n + 1)].bitcast(FP4X4),
+                    lhsT_scale=wg_s[:, P * n : P * (n + 1)],
+                    rhs=v_w[:].bitcast(FP8X4),
+                    rhs_scale=v_s[:],
+                    start=True,
+                    stop=True,
+                )
+                nc.scalar.copy(goal[b][:, t, :], acc[:])
+
+        x_w = [keep.tile([P, S], U32, name="x_w%d" % a, align_bytes=ALIGN) for a in range(2)]
+        x_s = [keep.tile([P, S], U8, name="x_s%d" % a, align_bytes=ALIGN) for a in range(2)]
+
+        def picks(a, engines):
+            picked = stage.tile([P, PACK, S], F32, name="picked")
+            for i in range(PACK):
+                nc.vector.tensor_tensor(picked[:, i, :], x_planes[(a, i)][:].indirect(head_lists[:]), wgt_sb[:], MULT)
+            woven = stage.tile([P, S, PACK], BF16, name="woven", align_bytes=ALIGN)
+            for u, engine in enumerate(engines):
+                cols = slice(u * S // 2, (u + 1) * S // 2)
+                cast_copy(
+                    engine,
+                    woven[:, cols, :].rearrange("p (c e) i -> p c i e", e=4),
+                    picked[:, :, cols].rearrange("p i (c e) -> p c i e", e=4),
+                )
+            nc.vector.quantize_mx(out=x_w[a][:].bitcast(FP8X4), scales=x_s[a][:], in_=woven[:].rearrange("p j i -> p (j i)"))
+
+        w_w, w_s = {}, {}
+
+        def convert(key, engines):
+            raw = raw_w[key]
+            w_w[key] = keep.tile([P, KP], U32, name="w_w_%s%d%d" % key, align_bytes=ALIGN)
+            w_s[key] = keep.tile([P, KP], U8, name="w_s_%s%d%d" % key, align_bytes=ALIGN)
+            for u, engine in enumerate(engines):
+                half = halves.tile([P, 2, P, PACK], BF16, name="half", align_bytes=ALIGN)
+                cast_copy(
+                    engine,
+                    half[:].rearrange("p t m j -> p m j t"),
+                    raw[:].rearrange("p j (m t) -> p m j t", t=PACK)[:, :, :, 2 * u : 2 * u + 2],
+                )
+                cols = slice(2 * P * u, 2 * P * (u + 1))
+                nc.vector.quantize_mx(
+                    out=w_w[key][:, cols].bitcast(FP8X4),
+                    scales=w_s[key][:, cols],
+                    in_=half[:].rearrange("p t m j -> p (t m j)"),
+                )
+
+        def project(name, b, first_bank):
+            accs = [bank(first_bank + t, [P, S]) for t in range(PACK)]
+            for a in range(2):
+                for t in range(PACK):
+                    cols = slice(P * t, P * (t + 1))
+                    nc.tensor.matmul_mx(
+                        out=accs[t][:],
+                        lhsT=w_w[(name, b, a)][:, cols].bitcast(FP8X4),
+                        lhsT_scale=w_s[(name, b, a)][:, cols],
+                        rhs=x_w[a][:].bitcast(FP8X4),
+                        rhs_scale=x_s[a][:],
+                        start=(a == 0),
+                        stop=(a == 1),
+                    )
+            return accs
+
+        def gate(b, logits):
+            gated = keep.tile([P, PACK, S], F32, name="gated%d" % b)
+            for t in range(PACK):
+                nc.scalar.activation(gated[:, t, :], logits[t][:], SIGMOID, bias=bb_sb[:, b, t : t + 1])
+            return gated
+
+        def apply_gate(feats, gated):
+            for t in range(PACK):
+                nc.vector.tensor_tensor(gated[:, t, :], feats[t][:], gated[:, t, :], MULT)
+
+        h_w = [keep.tile([P, S], U32, name="h_w%d" % b, align_bytes=ALIGN) for b in range(2)]
+        h_s = [keep.tile([P, S], U8, name="h_s%d" % b, align_bytes=ALIGN) for b in range(2)]
+
+        def add_goal(b, gated, cols):
+            width = cols.stop - cols.start
+            h = halves.tile([P, width, PACK], BF16, name="half", align_bytes=ALIGN)
+            nc.vector.tensor_tensor(
+                h[:].rearrange("p (c e) t -> p c t e", e=4),
+                gated[:, :, cols].rearrange("p t (c e) -> p c t e", e=4),
+                goal[b][:, :, cols].rearrange("p t (c e) -> p c t e", e=4),
+                ADD,
+            )
+            return h
+
+        def quantize_h(b, h, cols):
+            nc.vector.quantize_mx(out=h_w[b][:, cols].bitcast(FP8X4), scales=h_s[b][:, cols], in_=h[:].rearrange("p j t -> p (j t)"))
+
+        picks(0, "SS")
+        picks(1, "SV")
+        convert(("b", 0, 0), "VS")
+        convert(("b", 0, 1), "VS")
+        gated0 = gate(0, project("b", 0, 0))
+        convert(("a", 0, 0), "VV")
+        convert(("a", 0, 1), "VS")
+        apply_gate(project("a", 0, 4), gated0)
+        convert(("b", 1, 0), "SS")
+        convert(("b", 1, 1), "VS")
+        logits1 = project("b", 1, 0)
+        convert(("a", 1, 0), "SS")
+        convert(("a", 1, 1), "VS")
+        gated1 = gate(1, logits1)
+        parts = [slice(0, S // 2), slice(S // 2, S)]
+        h0 = [add_goal(0, gated0, cols) for cols in parts]
+        for h, cols in zip(h0, parts):
+            quantize_h(0, h, cols)
+        apply_gate(project("a", 1, 4), gated1)
+
+        out_rows = out.rearrange("(h p) j -> p h j", p=P)
+        chunks = [slice(c, c + TAIL) for c in range(0, S, TAIL)]
+
+        def value_pass(acc, u, b, cols):
+            nc.tensor.matmul_mx(
+                out=acc[:],
+                lhsT=wv_w[:, b, P * u : P * (u + 1)].bitcast(FP8X4),
+                lhsT_scale=wv_s[:, b, P * u : P * (u + 1)],
+                rhs=h_w[b][:, cols].bitcast(FP8X4),
+                rhs_scale=h_s[b][:, cols],
+                start=(b == 0),
+                stop=(b == 1),
+            )
+
+        values = {(c, u): bank(4 * u + c, [P, TAIL]) for u in range(2) for c in range(len(chunks))}
+        for u in range(2):
+            for c, cols in enumerate(chunks):
+                value_pass(values[(c, u)], u, 0, cols)
+        h1 = add_goal(1, gated1, chunks[0])
+        for c, cols in enumerate(chunks):
+            h_now = h1
+            last = c + 1 == len(chunks)
+            if not last:
+                h1 = add_goal(1, gated1, chunks[c + 1])
+            quantize_h(1, h_now, cols)
+            result = stage.tile([P, 2, TAIL], F32, name="result", bufs=4)
+            for u in range(2):
+                value_pass(values[(c, u)], u, 1, cols)
+            nc.scalar.activation(result[:, 0, :], values[(c, 0)][:], IDENTITY, bias=bv_sb[:, 0:1])
+            if last:
+                nc.vector.tensor_scalar_add(result[:, 1, :], values[(c, 1)][:], bv_sb[:, 1:2])
+            else:
+                nc.scalar.activation(result[:, 1, :], values[(c, 1)][:], IDENTITY, bias=bv_sb[:, 1:2])
+            nc.sync.dma_start(out_rows[:, :, cols], result[:])

@@ -71,8 +71,8 @@ def tile_list_replay_goal_value_kernel(
             nc.sync.dma_start(plane[:], rows[:, i, :])
             return plane
 
-        def load_w(w, b, a):
-            raw = big.tile([P, PACK, KP], F32, name="big")
+        def load_w(w, b, a, pool, tag):
+            raw = pool.tile([P, PACK, KP], F32, name=tag)
             src = w[a * KP : (a + 1) * KP, b * KP : (b + 1) * KP]
             nc.sync.dma_start(raw[:], src.rearrange("(p j) c -> p j c", j=PACK))
             return raw
@@ -103,7 +103,8 @@ def tile_list_replay_goal_value_kernel(
         for b in range(2):
             for name, w in (("b", wb), ("a", wa)):
                 for a in range(2):
-                    raw_w[(name, b, a)] = load_w(w, b, a)
+                    own = (name, b, a) == ("a", 1, 1)
+                    raw_w[(name, b, a)] = load_w(w, b, a, keep if own else big, "gated1" if own else "big")
         nc.sync.dma_start(wv_w[:].bitcast(I32), wv_words.rearrange("a p e i -> p a (e i)").bitcast(I32))
 
         v_w = keep.tile([P, S], U32, name="v_w", align_bytes=ALIGN)
@@ -159,14 +160,15 @@ def tile_list_replay_goal_value_kernel(
             raw = raw_w[key]
             w_w[key] = keep.tile([P, KP], U32, name="w_w_%s%d%d" % key, align_bytes=ALIGN)
             w_s[key] = keep.tile([P, KP], U8, name="w_s_%s%d%d" % key, align_bytes=ALIGN)
+            share = PACK // len(engines)
             for u, engine in enumerate(engines):
-                half = halves.tile([P, 2, P, PACK], BF16, name="half", align_bytes=ALIGN)
+                half = halves.tile([P, share, P, PACK], BF16, name="half", align_bytes=ALIGN)
                 cast_copy(
                     engine,
                     half[:].rearrange("p t m j -> p m j t"),
-                    raw[:].rearrange("p j (m t) -> p m j t", t=PACK)[:, :, :, 2 * u : 2 * u + 2],
+                    raw[:].rearrange("p j (m t) -> p m j t", t=PACK)[:, :, :, share * u : share * (u + 1)],
                 )
-                cols = slice(2 * P * u, 2 * P * (u + 1))
+                cols = slice(share * P * u, share * P * (u + 1))
                 nc.vector.quantize_mx(
                     out=w_w[key][:, cols].bitcast(FP8X4),
                     scales=w_s[key][:, cols],
@@ -202,38 +204,35 @@ def tile_list_replay_goal_value_kernel(
         h_w = [keep.tile([P, S], U32, name="h_w%d" % b, align_bytes=ALIGN) for b in range(2)]
         h_s = [keep.tile([P, S], U8, name="h_s%d" % b, align_bytes=ALIGN) for b in range(2)]
 
-        def add_goal(b, gated, cols):
-            width = cols.stop - cols.start
-            h = halves.tile([P, width, PACK], BF16, name="half", align_bytes=ALIGN)
+        def add_goal(b, gated, cols, h):
             nc.vector.tensor_tensor(
-                h[:].rearrange("p (c e) t -> p c t e", e=4),
+                h.rearrange("p (c e) t -> p c t e", e=4),
                 gated[:, :, cols].rearrange("p t (c e) -> p c t e", e=4),
                 goal[b][:, :, cols].rearrange("p t (c e) -> p c t e", e=4),
                 ADD,
             )
-            return h
 
         def quantize_h(b, h, cols):
-            nc.vector.quantize_mx(out=h_w[b][:, cols].bitcast(FP8X4), scales=h_s[b][:, cols], in_=h[:].rearrange("p j t -> p (j t)"))
+            nc.vector.quantize_mx(out=h_w[b][:, cols].bitcast(FP8X4), scales=h_s[b][:, cols], in_=h.rearrange("p j t -> p (j t)"))
 
         picks(0, "SS")
         picks(1, "SV")
         convert(("b", 0, 0), "VS")
         convert(("b", 0, 1), "VS")
         gated0 = gate(0, project("b", 0, 0))
-        convert(("a", 0, 0), "VV")
-        convert(("a", 0, 1), "VS")
+        convert(("a", 0, 0), "V")
+        convert(("a", 0, 1), "VV")
         apply_gate(project("a", 0, 4), gated0)
-        convert(("b", 1, 0), "SS")
-        convert(("b", 1, 1), "VS")
+        h0 = halves.tile([P, S, PACK], BF16, name="h0", bufs=1, align_bytes=ALIGN)
+        convert(("b", 1, 0), "S")
+        for cols in (slice(0, S // 2), slice(S // 2, S)):
+            add_goal(0, gated0, cols, h0[:, cols, :])
+        convert(("b", 1, 1), "S")
         logits1 = project("b", 1, 0)
-        convert(("a", 1, 0), "SS")
+        convert(("a", 1, 0), "S")
         convert(("a", 1, 1), "VS")
         gated1 = gate(1, logits1)
-        parts = [slice(0, S // 2), slice(S // 2, S)]
-        h0 = [add_goal(0, gated0, cols) for cols in parts]
-        for h, cols in zip(h0, parts):
-            quantize_h(0, h, cols)
+        quantize_h(0, h0[:], slice(0, S))
         apply_gate(project("a", 1, 4), gated1)
 
         out_rows = out.rearrange("(h p) j -> p h j", p=P)
@@ -241,32 +240,28 @@ def tile_list_replay_goal_value_kernel(
 
         def value_pass(acc, u, b, cols):
             nc.tensor.matmul_mx(
-                out=acc[:],
+                out=acc[:, u, :],
                 lhsT=wv_w[:, b, P * u : P * (u + 1)].bitcast(FP8X4),
                 lhsT_scale=wv_s[:, b, P * u : P * (u + 1)],
                 rhs=h_w[b][:, cols].bitcast(FP8X4),
                 rhs_scale=h_s[b][:, cols],
-                start=(b == 0),
-                stop=(b == 1),
+                start=(b == 0 and u == 0),
+                stop=(b == 1 and u == 1),
             )
 
-        values = {(c, u): bank(4 * u + c, [P, TAIL]) for u in range(2) for c in range(len(chunks))}
-        for u in range(2):
-            for c, cols in enumerate(chunks):
-                value_pass(values[(c, u)], u, 0, cols)
-        h1 = add_goal(1, gated1, chunks[0])
+        values = [bank(4 + c, [P, 2, TAIL]) for c in range(len(chunks))]
         for c, cols in enumerate(chunks):
-            h_now = h1
-            last = c + 1 == len(chunks)
-            if not last:
-                h1 = add_goal(1, gated1, chunks[c + 1])
-            quantize_h(1, h_now, cols)
+            for u in range(2):
+                value_pass(values[c], u, 0, cols)
+        h1 = [halves.tile([P, TAIL, PACK], BF16, name="h1_%d" % c, bufs=1, align_bytes=ALIGN) for c in range(len(chunks))]
+        add_goal(1, gated1, chunks[0], h1[0][:])
+        for c, cols in enumerate(chunks):
+            if c + 1 < len(chunks):
+                add_goal(1, gated1, chunks[c + 1], h1[c + 1][:])
+            quantize_h(1, h1[c][:], cols)
             result = stage.tile([P, 2, TAIL], F32, name="result", bufs=4)
             for u in range(2):
-                value_pass(values[(c, u)], u, 1, cols)
-            nc.scalar.activation(result[:, 0, :], values[(c, 0)][:], IDENTITY, bias=bv_sb[:, 0:1])
-            if last:
-                nc.vector.tensor_scalar_add(result[:, 1, :], values[(c, 1)][:], bv_sb[:, 1:2])
-            else:
-                nc.scalar.activation(result[:, 1, :], values[(c, 1)][:], IDENTITY, bias=bv_sb[:, 1:2])
+                value_pass(values[c], u, 1, cols)
+            for u in range(2):
+                nc.scalar.activation(result[:, u, :], values[c][:, u, :], IDENTITY, bias=bv_sb[:, u : u + 1])
             nc.sync.dma_start(out_rows[:, :, cols], result[:])

@@ -57,13 +57,10 @@ def tile_list_replay_goal_value_kernel(
         wgt_sb = keep.tile([P, S], F32, name="wgt_sb")
         bb_sb = keep.tile([P, 2, PACK], F32, name="bb_sb")
         bv_sb = keep.tile([P, 2], F32, name="bv_sb")
-        warm = keep.tile([P, 2], F32, name="warm")
 
         nc.vector.memset(tab_s[:].bitcast(I32), 0)
         nc.vector.memset(wg_raw_s[:].bitcast(I32), 0)
         nc.vector.memset(wv_s[:].rearrange("p a e -> p (a e)").bitcast(I32), 0)
-        nc.vector.memset(warm[:, 0:1], 0.0)
-        nc.scalar.activation(warm[:, 1:2], warm[:, 0:1], SIGMOID)
 
         def load_x(a, i):
             plane = big.tile([P, T], F32, name="big")
@@ -79,26 +76,18 @@ def tile_list_replay_goal_value_kernel(
 
         nc.sync.dma_start(goal_list[:], offs)
         nc.sync.dma_start(tab_w[:].bitcast(I32), tab_words[0].rearrange("p t i -> p (t i)").bitcast(I32))
-        for q in range(4):
-            nc.sync.dma_start(tab_s[32 * q : 32 * q + 4, :].bitcast(I32), tab_scales[0, 4 * q : 4 * q + 4, :].bitcast(I32))
+        for r in range(4):
+            nc.sync.dma_start(tab_s[r:P:32, :].bitcast(I32), tab_scales[0, r:16:4, :].bitcast(I32))
         nc.sync.dma_start(wg_raw_w[:].bitcast(I32), wg_words[0].bitcast(I32))
         x_planes = {(0, 0): load_x(0, 0)}
-        for q in range(4):
-            nc.sync.dma_start(wg_raw_s[32 * q : 32 * q + 4, :].bitcast(I32), wg_scales[0, 4 * q : 4 * q + 4, :].bitcast(I32))
+        for r in range(4):
+            nc.sync.dma_start(wg_raw_s[r:P:32, :].bitcast(I32), wg_scales[0, r:16:4, :].bitcast(I32))
         nc.sync.dma_start(head_lists[:], offs2)
         nc.sync.dma_start(wgt_sb[:], wgt)
         for n in range(1, 8):
             x_planes[(n // 4, n % 4)] = load_x(n // 4, n % 4)
             if n == 2:
                 nc.sync.dma_start(bb_sb[:], bb.rearrange("(b p t) -> p b t", p=P, t=PACK))
-                with nc.allow_non_contiguous_dma(reason="one bias value for each partition and half"):
-                    nc.sync.dma_start(bv_sb[:], bv.rearrange("(h p) -> p h", p=P))
-            if n == 4:
-                for q in range(4):
-                    nc.sync.dma_start(
-                        wv_s[32 * q : 32 * q + 4, :, :].bitcast(I32),
-                        wv_scales[:, 4 * q : 4 * q + 4, :].rearrange("a q e -> q a e").bitcast(I32),
-                    )
         raw_w = {}
         for b in range(2):
             for name, w in (("b", wb), ("a", wa)):
@@ -106,6 +95,12 @@ def tile_list_replay_goal_value_kernel(
                     own = (name, b, a) == ("a", 1, 1)
                     raw_w[(name, b, a)] = load_w(w, b, a, keep if own else big, "gated1" if own else "big")
         nc.sync.dma_start(wv_w[:].bitcast(I32), wv_words.rearrange("a p e i -> p a (e i)").bitcast(I32))
+        for r in range(4):
+            nc.sync.dma_start(
+                wv_s[r:P:32, :, :].bitcast(I32), wv_scales[:, r:16:4, :].rearrange("a q e -> q a e").bitcast(I32)
+            )
+        with nc.allow_non_contiguous_dma(reason="one bias value for each partition and half"):
+            nc.sync.dma_start(bv_sb[:], bv.rearrange("(h p) -> p h", p=P))
 
         v_w = keep.tile([P, S], U32, name="v_w", align_bytes=ALIGN)
         v_s = keep.tile([P, S], U8, name="v_s", align_bytes=ALIGN)

@@ -92,7 +92,7 @@ def tile_list_replay_goal_value_kernel(
         for b in range(2):
             for name, w in (("b", wb), ("a", wa)):
                 for a in range(2):
-                    own = (name, b, a) == ("a", 1, 1)
+                    own = (name, b, a) == ("a", 1, 0)
                     raw_w[(name, b, a)] = load_w(w, b, a, keep if own else big, "gated1" if own else "big")
         nc.sync.dma_start(wv_w[:].bitcast(I32), wv_words.rearrange("a p e i -> p a (e i)").bitcast(I32))
         for r in range(4):
@@ -172,8 +172,8 @@ def tile_list_replay_goal_value_kernel(
 
         def project(name, b, first_bank):
             accs = [bank(first_bank + t, [P, S]) for t in range(PACK)]
-            for a in range(2):
-                for t in range(PACK):
+            for t in range(PACK):
+                for a in range(2):
                     cols = slice(P * t, P * (t + 1))
                     nc.tensor.matmul_mx(
                         out=accs[t][:],
@@ -219,13 +219,13 @@ def tile_list_replay_goal_value_kernel(
         convert(("a", 0, 1), "VV")
         apply_gate(project("a", 0, 4), gated0)
         h0 = halves.tile([P, S, PACK], BF16, name="h0", bufs=1, align_bytes=ALIGN)
+        add_goal(0, gated0, slice(0, S // 2), h0[:, : S // 2, :])
         convert(("b", 1, 0), "S")
-        for cols in (slice(0, S // 2), slice(S // 2, S)):
-            add_goal(0, gated0, cols, h0[:, cols, :])
+        add_goal(0, gated0, slice(S // 2, S), h0[:, S // 2 :, :])
         convert(("b", 1, 1), "S")
         logits1 = project("b", 1, 0)
-        convert(("a", 1, 0), "S")
-        convert(("a", 1, 1), "VS")
+        convert(("a", 1, 0), "SS")
+        convert(("a", 1, 1), "VV")
         gated1 = gate(1, logits1)
         quantize_h(0, h0[:], slice(0, S))
         apply_gate(project("a", 1, 4), gated1)

@@ -38,9 +38,9 @@ def tile_list_replay_goal_value_kernel(
 
     with ExitStack() as ctx:
         keep = ctx.enter_context(tc.tile_pool(name="keep", bufs=1))
-        big = ctx.enter_context(tc.tile_pool(name="big", bufs=10))
+        big = ctx.enter_context(tc.tile_pool(name="big", bufs=9))
         stage = ctx.enter_context(tc.tile_pool(name="stage", bufs=2))
-        halves = ctx.enter_context(tc.tile_pool(name="halves", bufs=6))
+        halves = ctx.enter_context(tc.tile_pool(name="halves", bufs=4))
         psum = ctx.enter_context(tc.psum_pool(name="psum", bufs=1))
 
         def bank(n, shape):
@@ -58,19 +58,22 @@ def tile_list_replay_goal_value_kernel(
         bb_sb = keep.tile([P, 2, PACK], F32, name="bb_sb")
         bv_sb = keep.tile([P, 2], F32, name="bv_sb")
 
+        warm = keep.tile([P, 2], F32, name="warm")
+        nc.vector.memset(warm[:, 0:1], 0.0)
+        nc.scalar.activation(warm[:, 1:2], warm[:, 0:1], SIGMOID)
         nc.vector.memset(tab_s[:].bitcast(I32), 0)
         nc.vector.memset(wg_raw_s[:].bitcast(I32), 0)
         nc.vector.memset(wv_s[:].rearrange("p a e -> p (a e)").bitcast(I32), 0)
 
         def load_x(a, i):
-            plane = big.tile([P, T], F32, name="big")
+            plane = keep.tile([P, T], F32, name="last_plane", align_bytes=ALIGN) if (a, i) == (1, 3) else big.tile([P, T], F32, name="big")
             rows = xT[a * KP : (a + 1) * KP, :].rearrange("(p i) t -> p i t", i=PACK)
             nc.sync.dma_start(plane[:], rows[:, i, :])
             return plane
 
-        def load_w(w, b, a, pool, tag):
-            raw = pool.tile([P, PACK, KP], F32, name=tag)
-            src = w[a * KP : (a + 1) * KP, b * KP : (b + 1) * KP]
+        def load_w(w, b, a, pool, tag, first=0, width=KP):
+            raw = pool.tile([P, PACK, width], F32, name=tag)
+            src = w[a * KP : (a + 1) * KP, b * KP + first : b * KP + first + width]
             nc.sync.dma_start(raw[:], src.rearrange("(p j) c -> p j c", j=PACK))
             return raw
 
@@ -84,16 +87,22 @@ def tile_list_replay_goal_value_kernel(
             nc.sync.dma_start(wg_raw_s[r:P:32, :].bitcast(I32), wg_scales[0, r:16:4, :].bitcast(I32))
         nc.sync.dma_start(head_lists[:], offs2)
         nc.sync.dma_start(wgt_sb[:], wgt)
+        raw_w = {}
         for n in range(1, 8):
+            if n == 5:
+                raw_w[("b", 0, 0)] = [load_w(wb, 0, 0, big, "big")]
             x_planes[(n // 4, n % 4)] = load_x(n // 4, n % 4)
             if n == 2:
                 nc.sync.dma_start(bb_sb[:], bb.rearrange("(b p t) -> p b t", p=P, t=PACK))
-        raw_w = {}
         for b in range(2):
             for name, w in (("b", wb), ("a", wa)):
                 for a in range(2):
-                    own = (name, b, a) == ("a", 1, 0)
-                    raw_w[(name, b, a)] = load_w(w, b, a, keep if own else big, "gated1" if own else "big")
+                    if (name, a) == ("a", 1):
+                        raw_w[(name, b, a)] = [load_w(w, b, a, keep, "gated1" if (b, u) == (1, 0) else "piece%d%d" % (b, u), u * KP // 2, KP // 2) for u in range(2)]
+                    elif (name, b) == ("a", 0):
+                        raw_w[(name, b, a)] = [load_w(w, b, a, keep, "gated%d" % b)]
+                    elif (name, b, a) != ("b", 0, 0):
+                        raw_w[(name, b, a)] = [load_w(w, b, a, big, "big")]
         nc.sync.dma_start(wv_w[:].bitcast(I32), wv_words.rearrange("a p e i -> p a (e i)").bitcast(I32))
         for r in range(4):
             nc.sync.dma_start(
@@ -135,10 +144,12 @@ def tile_list_replay_goal_value_kernel(
         x_w = [keep.tile([P, S], U32, name="x_w%d" % a, align_bytes=ALIGN) for a in range(2)]
         x_s = [keep.tile([P, S], U8, name="x_s%d" % a, align_bytes=ALIGN) for a in range(2)]
 
-        def picks(a, engines):
+        def picks(a, engines, between=None):
             picked = stage.tile([P, PACK, S], F32, name="picked")
             for i in range(PACK):
                 nc.vector.tensor_tensor(picked[:, i, :], x_planes[(a, i)][:].indirect(head_lists[:]), wgt_sb[:], MULT)
+            if between:
+                between()
             woven = stage.tile([P, S, PACK], BF16, name="woven", align_bytes=ALIGN)
             for u, engine in enumerate(engines):
                 cols = slice(u * S // 2, (u + 1) * S // 2)
@@ -151,40 +162,46 @@ def tile_list_replay_goal_value_kernel(
 
         w_w, w_s = {}, {}
 
-        def convert(key, engines):
-            raw = raw_w[key]
-            w_w[key] = keep.tile([P, KP], U32, name="w_w_%s%d%d" % key, align_bytes=ALIGN)
-            w_s[key] = keep.tile([P, KP], U8, name="w_s_%s%d%d" % key, align_bytes=ALIGN)
-            share = PACK // len(engines)
-            for u, engine in enumerate(engines):
-                half = halves.tile([P, share, P, PACK], BF16, name="half", align_bytes=ALIGN)
-                cast_copy(
-                    engine,
-                    half[:].rearrange("p t m j -> p m j t"),
-                    raw[:].rearrange("p j (m t) -> p m j t", t=PACK)[:, :, :, share * u : share * (u + 1)],
-                )
-                cols = slice(share * P * u, share * P * (u + 1))
-                nc.vector.quantize_mx(
-                    out=w_w[key][:, cols].bitcast(FP8X4),
-                    scales=w_s[key][:, cols],
-                    in_=half[:].rearrange("p t m j -> p (t m j)"),
+        rounded = {}
+
+        def cast(key, engine, first, last, t0=0, t1=PACK):
+            if key not in rounded:
+                rounded[key] = halves.tile([P, PACK, P, PACK], BF16, name="half", align_bytes=ALIGN)
+            per_piece = P // len(raw_w[key])
+            raw = raw_w[key][first // per_piece]
+            at = first % per_piece
+            cast_copy(
+                engine,
+                rounded[key][:, t0:t1].rearrange("p t m j -> p m j t")[:, first:last],
+                raw[:].rearrange("p j (m t) -> p m j t", t=PACK)[:, at : at + last - first, :, t0:t1],
+            )
+
+        def quantize_w(key, first=0, last=PACK):
+            if key not in w_w:
+                w_w[key] = keep.tile([P, KP], U32, name="last_plane" if key == ("b", 0, 0) else "w_w_%s%d%d" % key, align_bytes=ALIGN)
+                w_s[key] = keep.tile([P, KP], U8, name="w_s_%s%d%d" % key, align_bytes=ALIGN)
+            cols = slice(P * first, P * last)
+            nc.vector.quantize_mx(
+                out=w_w[key][:, cols].bitcast(FP8X4),
+                scales=w_s[key][:, cols],
+                in_=rounded[key][:, first:last].rearrange("p t m j -> p (t m j)"),
+            )
+
+        def project(name, b, a, accs, tiles=range(PACK)):
+            for t in tiles:
+                cols = slice(P * t, P * (t + 1))
+                nc.tensor.matmul_mx(
+                    out=accs[t][:],
+                    lhsT=w_w[(name, b, a)][:, cols].bitcast(FP8X4),
+                    lhsT_scale=w_s[(name, b, a)][:, cols],
+                    rhs=x_w[a][:].bitcast(FP8X4),
+                    rhs_scale=x_s[a][:],
+                    start=(a == 0),
+                    stop=(a == 1),
                 )
 
-        def project(name, b, first_bank):
-            accs = [bank(first_bank + t, [P, S]) for t in range(PACK)]
-            for t in range(PACK):
-                for a in range(2):
-                    cols = slice(P * t, P * (t + 1))
-                    nc.tensor.matmul_mx(
-                        out=accs[t][:],
-                        lhsT=w_w[(name, b, a)][:, cols].bitcast(FP8X4),
-                        lhsT_scale=w_s[(name, b, a)][:, cols],
-                        rhs=x_w[a][:].bitcast(FP8X4),
-                        rhs_scale=x_s[a][:],
-                        start=(a == 0),
-                        stop=(a == 1),
-                    )
-            return accs
+        def banks(first):
+            return [bank(first + t, [P, S]) for t in range(PACK)]
 
         def gate(b, logits):
             gated = keep.tile([P, PACK, S], F32, name="gated%d" % b)
@@ -210,53 +227,88 @@ def tile_list_replay_goal_value_kernel(
         def quantize_h(b, h, cols):
             nc.vector.quantize_mx(out=h_w[b][:, cols].bitcast(FP8X4), scales=h_s[b][:, cols], in_=h.rearrange("p j t -> p (j t)"))
 
+        b00, b01, a00, a01 = ("b", 0, 0), ("b", 0, 1), ("a", 0, 0), ("a", 0, 1)
+        b10, b11, a10, a11 = ("b", 1, 0), ("b", 1, 1), ("a", 1, 0), ("a", 1, 1)
         picks(0, "SS")
-        picks(1, "SV")
-        convert(("b", 0, 0), "VS")
-        convert(("b", 0, 1), "VS")
-        gated0 = gate(0, project("b", 0, 0))
-        convert(("a", 0, 0), "V")
-        convert(("a", 0, 1), "VV")
-        apply_gate(project("a", 0, 4), gated0)
+        cast(b00, "S", 0, 128)
+        picks(1, "SV", lambda: quantize_w(b00))
+        logits = banks(0)
+        project("b", 0, 0, logits)
+        cast(b01, "V", 0, 128, 0, 2)
+        cast(b01, "S", 0, 128, 2, 4)
+        quantize_w(b01)
+        project("b", 0, 1, logits)
+        cast(a00, "V", 0, 128, 0, 2)
+        cast(a00, "S", 0, 128, 2, 4)
+        gated0 = gate(0, logits)
+        quantize_w(a00)
+        feats = banks(4)
+        project("a", 0, 0, feats)
+        cast(a01, "V", 0, 64)
+        cast(a01, "V", 64, 128)
+        quantize_w(a01, 0, 2)
+        quantize_w(a01, 2, 4)
+        project("a", 0, 1, feats)
+        apply_gate(feats, gated0)
         h0 = halves.tile([P, S, PACK], BF16, name="h0", bufs=1, align_bytes=ALIGN)
+        cast(b10, "S", 0, 128)
+        quantize_w(b10)
+        logits = banks(0)
+        project("b", 1, 0, logits)
         add_goal(0, gated0, slice(0, S // 2), h0[:, : S // 2, :])
-        convert(("b", 1, 0), "S")
         add_goal(0, gated0, slice(S // 2, S), h0[:, S // 2 :, :])
-        convert(("b", 1, 1), "S")
-        logits1 = project("b", 1, 0)
-        convert(("a", 1, 0), "SS")
-        convert(("a", 1, 1), "VV")
-        gated1 = gate(1, logits1)
-        quantize_h(0, h0[:], slice(0, S))
-        apply_gate(project("a", 1, 4), gated1)
+        cast(b11, "S", 0, 128)
+        quantize_w(b11)
+        project("b", 1, 1, logits)
+        cast(a10, "V", 0, 128, 0, 2)
+        cast(a10, "S", 0, 128, 2, 4)
+        quantize_w(a10)
+        feats = banks(4)
+        project("a", 1, 0, feats)
+        gated1 = gate(1, logits)
+        cast(a11, "S", 0, 64)
+        cast(a11, "V", 64, 128)
+        quantize_h(0, h0[:, : S // 2, :], slice(0, S // 2))
+        quantize_w(a11, 0, 2)
+        quantize_w(a11, 2, 4)
+        quantize_h(0, h0[:, S // 2 :, :], slice(S // 2, S))
+        project("a", 1, 1, feats)
+        apply_gate(feats, gated1)
 
         out_rows = out.rearrange("(h p) j -> p h j", p=P)
         chunks = [slice(c, c + TAIL) for c in range(0, S, TAIL)]
 
         def value_pass(acc, u, b, cols):
             nc.tensor.matmul_mx(
-                out=acc[:, u, :],
+                out=acc[:],
                 lhsT=wv_w[:, b, P * u : P * (u + 1)].bitcast(FP8X4),
                 lhsT_scale=wv_s[:, b, P * u : P * (u + 1)],
                 rhs=h_w[b][:, cols].bitcast(FP8X4),
                 rhs_scale=h_s[b][:, cols],
-                start=(b == 0 and u == 0),
-                stop=(b == 1 and u == 1),
+                start=(b == 0),
+                stop=(b == 1),
             )
 
-        values = [bank(4 + c, [P, 2, TAIL]) for c in range(len(chunks))]
-        for c, cols in enumerate(chunks):
-            for u in range(2):
-                value_pass(values[c], u, 0, cols)
+        values = [[bank(c + 4 * u, [P, TAIL]) for u in range(2)] for c in range(len(chunks))]
+        for u in range(2):
+            for c, cols in enumerate(chunks):
+                value_pass(values[c][u], u, 0, cols)
         h1 = [halves.tile([P, TAIL, PACK], BF16, name="h1_%d" % c, bufs=1, align_bytes=ALIGN) for c in range(len(chunks))]
         add_goal(1, gated1, chunks[0], h1[0][:])
         for c, cols in enumerate(chunks):
             if c + 1 < len(chunks):
                 add_goal(1, gated1, chunks[c + 1], h1[c + 1][:])
             quantize_h(1, h1[c][:], cols)
-            result = stage.tile([P, 2, TAIL], F32, name="result", bufs=4)
             for u in range(2):
-                value_pass(values[c], u, 1, cols)
-            for u in range(2):
-                nc.scalar.activation(result[:, u, :], values[c][:, u, :], IDENTITY, bias=bv_sb[:, u : u + 1])
-            nc.sync.dma_start(out_rows[:, :, cols], result[:])
+                value_pass(values[c][u], u, 1, cols)
+            if c + 1 < len(chunks):
+                result = stage.tile([P, 2, TAIL], F32, name="result", bufs=3)
+                for u in range(2):
+                    nc.scalar.activation(result[:, u, :], values[c][u][:], IDENTITY, bias=bv_sb[:, u : u + 1])
+                nc.sync.dma_start(out_rows[:, :, cols], result[:])
+            else:
+                last = [stage.tile([P, TAIL], F32, name="last%d" % u, bufs=1) for u in range(2)]
+                nc.scalar.activation(last[0][:], values[c][0][:], IDENTITY, bias=bv_sb[:, 0:1])
+                nc.vector.tensor_scalar_add(last[1][:], values[c][1][:], bv_sb[:, 1:2])
+                for u in range(2):
+                    nc.sync.dma_start(out_rows[:, u, cols], last[u][:])

@@ -1,6 +1,7 @@
 from contextlib import ExitStack
 
 import concourse.mybir as mybir
+from concourse.masks import make_identity
 
 KX, T, KG, TG, S, H, N = 1024, 2048, 512, 1024, 512, 1024, 256
 FLOPS = 2 * S * (2 * KX * H + KG * H + H * N)
@@ -23,6 +24,7 @@ PACK = 4
 KP = P * PACK
 ALIGN = 64
 TAIL = 128
+HEADS = 8
 
 
 def tile_list_replay_goal_value_kernel(
@@ -58,6 +60,8 @@ def tile_list_replay_goal_value_kernel(
         bb_sb = keep.tile([P, 2, PACK], F32, name="bb_sb")
         bv_sb = keep.tile([P, 2], F32, name="bv_sb")
 
+        wgt_rows = keep.tile([P, S], F32, name="wgt_rows")
+        nc.vector.memset(wgt_rows[:], 0.0)
         warm = keep.tile([P, 2], F32, name="warm")
         nc.vector.memset(warm[:, 0:1], 0.0)
         nc.scalar.activation(warm[:, 1:2], warm[:, 0:1], SIGMOID)
@@ -78,21 +82,23 @@ def tile_list_replay_goal_value_kernel(
             return raw
 
         nc.sync.dma_start(goal_list[:], offs)
+        nc.sync.dma_start(wgt_rows[0:HEADS, :], wgt[0 : P : P // HEADS, :])
         nc.sync.dma_start(tab_w[:].bitcast(I32), tab_words[0].rearrange("p t i -> p (t i)").bitcast(I32))
-        for r in range(4):
-            nc.sync.dma_start(tab_s[r:P:32, :].bitcast(I32), tab_scales[0, r:16:4, :].bitcast(I32))
-        nc.sync.dma_start(wg_raw_w[:].bitcast(I32), wg_words[0].bitcast(I32))
         x_planes = {(0, 0): load_x(0, 0)}
         for r in range(4):
-            nc.sync.dma_start(wg_raw_s[r:P:32, :].bitcast(I32), wg_scales[0, r:16:4, :].bitcast(I32))
+            nc.sync.dma_start(tab_s[r:P:32, :].bitcast(I32), tab_scales[0, r:16:4, :].bitcast(I32))
+        x_planes[(0, 1)] = load_x(0, 1)
         nc.sync.dma_start(head_lists[:], offs2)
-        nc.sync.dma_start(wgt_sb[:], wgt)
+        nc.sync.dma_start(wg_raw_w[:].bitcast(I32), wg_words[0].bitcast(I32))
+        x_planes[(0, 2)] = load_x(0, 2)
+        for r in range(4):
+            nc.sync.dma_start(wg_raw_s[r:P:32, :].bitcast(I32), wg_scales[0, r:16:4, :].bitcast(I32))
         raw_w = {}
-        for n in range(1, 8):
+        for n in range(3, 8):
             if n == 5:
                 raw_w[("b", 0, 0)] = [load_w(wb, 0, 0, big, "big")]
             x_planes[(n // 4, n % 4)] = load_x(n // 4, n % 4)
-            if n == 2:
+            if n == 3:
                 nc.sync.dma_start(bb_sb[:], bb.rearrange("(b p t) -> p b t", p=P, t=PACK))
         for b in range(2):
             for name, w in (("b", wb), ("a", wa)):
@@ -110,6 +116,18 @@ def tile_list_replay_goal_value_kernel(
             )
         with nc.allow_non_contiguous_dma(reason="one bias value for each partition and half"):
             nc.sync.dma_start(bv_sb[:], bv.rearrange("(h p) -> p h", p=P))
+
+        identity = keep.tile([P, P], F32, name="identity")
+        make_identity(nc, identity[:])
+        turned = bank(0, [P, S // P, P])
+        for c in range(S // P):
+            nc.tensor.transpose(turned[:, c, :], wgt_rows[:, P * c : P * (c + 1)], identity[:])
+        spread = keep.tile([P, S // P, HEADS, P // HEADS], F32, name="wgt_spread")
+        nc.scalar.copy(spread[:], turned[:, :, 0:HEADS].unsqueeze(3).to_broadcast([P, S // P, HEADS, P // HEADS]))
+        back = bank(1, [P, S // P, P])
+        for c in range(S // P):
+            nc.tensor.transpose(back[:, c, :], spread[:, c].rearrange("p g r -> p (g r)"), identity[:])
+        nc.scalar.copy(wgt_sb[:], back[:].rearrange("p c j -> p (c j)"))
 
         v_w = keep.tile([P, S], U32, name="v_w", align_bytes=ALIGN)
         v_s = keep.tile([P, S], U8, name="v_s", align_bytes=ALIGN)
@@ -271,9 +289,9 @@ def tile_list_replay_goal_value_kernel(
         quantize_h(0, h0[:, : S // 2, :], slice(0, S // 2))
         quantize_w(a11, 0, 2)
         quantize_w(a11, 2, 4)
-        quantize_h(0, h0[:, S // 2 :, :], slice(S // 2, S))
         project("a", 1, 1, feats)
         apply_gate(feats, gated1)
+        quantize_h(0, h0[:, S // 2 :, :], slice(S // 2, S))
 
         out_rows = out.rearrange("(h p) j -> p h j", p=P)
         chunks = [slice(c, c + TAIL) for c in range(0, S, TAIL)]

@@ -40,7 +40,7 @@ def tile_list_replay_goal_value_kernel(
 
     with ExitStack() as ctx:
         keep = ctx.enter_context(tc.tile_pool(name="keep", bufs=1))
-        big = ctx.enter_context(tc.tile_pool(name="big", bufs=9))
+        big = ctx.enter_context(tc.tile_pool(name="big", bufs=10))
         stage = ctx.enter_context(tc.tile_pool(name="stage", bufs=2))
         halves = ctx.enter_context(tc.tile_pool(name="halves", bufs=4))
         psum = ctx.enter_context(tc.psum_pool(name="psum", bufs=1))
@@ -60,6 +60,8 @@ def tile_list_replay_goal_value_kernel(
         bb_sb = keep.tile([P, 2, PACK], F32, name="bb_sb")
         bv_sb = keep.tile([P, 2], F32, name="bv_sb")
 
+        identity = keep.tile([P, P], F32, name="identity")
+        make_identity(nc, identity[:])
         wgt_rows = keep.tile([P, S], F32, name="wgt_rows")
         nc.vector.memset(wgt_rows[:], 0.0)
         warm = keep.tile([P, 2], F32, name="warm")
@@ -81,10 +83,11 @@ def tile_list_replay_goal_value_kernel(
             nc.sync.dma_start(raw[:], src.rearrange("(p j) c -> p j c", j=PACK))
             return raw
 
-        nc.sync.dma_start(goal_list[:], offs)
-        nc.sync.dma_start(wgt_rows[0:HEADS, :], wgt[0 : P : P // HEADS, :])
         nc.sync.dma_start(tab_w[:].bitcast(I32), tab_words[0].rearrange("p t i -> p (t i)").bitcast(I32))
+        nc.sync.dma_start(goal_list[:], offs)
         x_planes = {(0, 0): load_x(0, 0)}
+        nc.sync.dma_start(wgt_rows[0:HEADS, :], wgt[0 : P : P // HEADS, :])
+        nc.sync.dma_start(wgt_rows[HEADS : HEADS + 2, :], bb.rearrange("(b c) -> b c", b=2))
         for r in range(4):
             nc.sync.dma_start(tab_s[r:P:32, :].bitcast(I32), tab_scales[0, r:16:4, :].bitcast(I32))
         x_planes[(0, 1)] = load_x(0, 1)
@@ -98,14 +101,10 @@ def tile_list_replay_goal_value_kernel(
             if n == 5:
                 raw_w[("b", 0, 0)] = [load_w(wb, 0, 0, big, "big")]
             x_planes[(n // 4, n % 4)] = load_x(n // 4, n % 4)
-            if n == 3:
-                nc.sync.dma_start(bb_sb[:], bb.rearrange("(b p t) -> p b t", p=P, t=PACK))
         for b in range(2):
             for name, w in (("b", wb), ("a", wa)):
                 for a in range(2):
-                    if (name, a) == ("a", 1):
-                        raw_w[(name, b, a)] = [load_w(w, b, a, keep, "gated1" if (b, u) == (1, 0) else "piece%d%d" % (b, u), u * KP // 2, KP // 2) for u in range(2)]
-                    elif (name, b) == ("a", 0):
+                    if (name, b, a) in (("a", 0, 0), ("a", 1, 1)):
                         raw_w[(name, b, a)] = [load_w(w, b, a, keep, "gated%d" % b)]
                     elif (name, b, a) != ("b", 0, 0):
                         raw_w[(name, b, a)] = [load_w(w, b, a, big, "big")]
@@ -117,8 +116,6 @@ def tile_list_replay_goal_value_kernel(
         with nc.allow_non_contiguous_dma(reason="one bias value for each partition and half"):
             nc.sync.dma_start(bv_sb[:], bv.rearrange("(h p) -> p h", p=P))
 
-        identity = keep.tile([P, P], F32, name="identity")
-        make_identity(nc, identity[:])
         turned = bank(0, [P, S // P, P])
         for c in range(S // P):
             nc.tensor.transpose(turned[:, c, :], wgt_rows[:, P * c : P * (c + 1)], identity[:])
@@ -128,6 +125,11 @@ def tile_list_replay_goal_value_kernel(
         for c in range(S // P):
             nc.tensor.transpose(back[:, c, :], spread[:, c].rearrange("p g r -> p (g r)"), identity[:])
         nc.scalar.copy(wgt_sb[:], back[:].rearrange("p c j -> p (c j)"))
+
+        dealt = bank(2, [P, PACK, P])
+        for t in range(PACK):
+            nc.tensor.transpose(dealt[:, t, :], wgt_rows[:, t:S:PACK], identity[:])
+        nc.scalar.copy(bb_sb[:], dealt[:, :, HEADS : HEADS + 2].rearrange("p t b -> p b t"))
 
         v_w = keep.tile([P, S], U32, name="v_w", align_bytes=ALIGN)
         v_s = keep.tile([P, S], U8, name="v_s", align_bytes=ALIGN)
@@ -262,8 +264,8 @@ def tile_list_replay_goal_value_kernel(
         quantize_w(a00)
         feats = banks(4)
         project("a", 0, 0, feats)
-        cast(a01, "V", 0, 64)
-        cast(a01, "V", 64, 128)
+        cast(a01, "V", 0, 128, 0, 2)
+        cast(a01, "V", 0, 128, 2, 4)
         quantize_w(a01, 0, 2)
         quantize_w(a01, 2, 4)
         project("a", 0, 1, feats)
@@ -283,15 +285,15 @@ def tile_list_replay_goal_value_kernel(
         quantize_w(a10)
         feats = banks(4)
         project("a", 1, 0, feats)
+        cast(a11, "V", 0, 128, 0, 2)
+        cast(a11, "S", 0, 128, 2, 4)
         gated1 = gate(1, logits)
-        cast(a11, "S", 0, 64)
-        cast(a11, "V", 64, 128)
         quantize_h(0, h0[:, : S // 2, :], slice(0, S // 2))
         quantize_w(a11, 0, 2)
         quantize_w(a11, 2, 4)
+        quantize_h(0, h0[:, S // 2 :, :], slice(S // 2, S))
         project("a", 1, 1, feats)
         apply_gate(feats, gated1)
-        quantize_h(0, h0[:, S // 2 :, :], slice(S // 2, S))
 
         out_rows = out.rearrange("(h p) j -> p h j", p=P)
         chunks = [slice(c, c + TAIL) for c in range(0, S, TAIL)]

@@ -60,10 +60,10 @@ def tile_list_replay_goal_value_kernel(
         bb_sb = keep.tile([P, 2, PACK], F32, name="bb_sb")
         bv_sb = keep.tile([P, 2], F32, name="bv_sb")
 
+        wgt_rows = keep.tile([P, S], F32, name="wgt_rows")
+        nc.gpsimd.memset(wgt_rows[:], 0.0)
         identity = keep.tile([P, P], F32, name="identity")
         make_identity(nc, identity[:])
-        wgt_rows = keep.tile([P, S], F32, name="wgt_rows")
-        nc.vector.memset(wgt_rows[:], 0.0)
         warm = keep.tile([P, 2], F32, name="warm")
         nc.vector.memset(warm[:, 0:1], 0.0)
         nc.scalar.activation(warm[:, 1:2], warm[:, 0:1], SIGMOID)
@@ -84,14 +84,14 @@ def tile_list_replay_goal_value_kernel(
             return raw
 
         nc.sync.dma_start(tab_w[:].bitcast(I32), tab_words[0].rearrange("p t i -> p (t i)").bitcast(I32))
-        nc.sync.dma_start(goal_list[:], offs)
-        x_planes = {(0, 0): load_x(0, 0)}
         nc.sync.dma_start(wgt_rows[0:HEADS, :], wgt[0 : P : P // HEADS, :])
         nc.sync.dma_start(wgt_rows[HEADS : HEADS + 2, :], bb.rearrange("(b c) -> b c", b=2))
+        nc.sync.dma_start(head_lists[:], offs2)
+        x_planes = {(0, 0): load_x(0, 0)}
+        nc.sync.dma_start(goal_list[:], offs)
         for r in range(4):
             nc.sync.dma_start(tab_s[r:P:32, :].bitcast(I32), tab_scales[0, r:16:4, :].bitcast(I32))
         x_planes[(0, 1)] = load_x(0, 1)
-        nc.sync.dma_start(head_lists[:], offs2)
         nc.sync.dma_start(wg_raw_w[:].bitcast(I32), wg_words[0].bitcast(I32))
         x_planes[(0, 2)] = load_x(0, 2)
         for r in range(4):
@@ -125,41 +125,6 @@ def tile_list_replay_goal_value_kernel(
         for c in range(S // P):
             nc.tensor.transpose(back[:, c, :], spread[:, c].rearrange("p g r -> p (g r)"), identity[:])
         nc.scalar.copy(wgt_sb[:], back[:].rearrange("p c j -> p (c j)"))
-
-        dealt = bank(2, [P, PACK, P])
-        for t in range(PACK):
-            nc.tensor.transpose(dealt[:, t, :], wgt_rows[:, t:S:PACK], identity[:])
-        nc.scalar.copy(bb_sb[:], dealt[:, :, HEADS : HEADS + 2].rearrange("p t b -> p b t"))
-
-        v_w = keep.tile([P, S], U32, name="v_w", align_bytes=ALIGN)
-        v_s = keep.tile([P, S], U8, name="v_s", align_bytes=ALIGN)
-        nc.vector.tensor_copy(v_w[:], tab_w[:].indirect(goal_list[:]))
-        nc.vector.tensor_copy(v_s[:], tab_s[:].indirect(goal_list[:]))
-        wg_w = keep.tile([P, 2 * H], U8, name="wg_w", align_bytes=ALIGN)
-        wg_s = keep.tile([P, H], U8, name="wg_s", align_bytes=ALIGN)
-        nc.vector.tensor_copy(
-            wg_w[:].bitcast(U16).rearrange("p (b t m) -> p b m t", b=2, t=PACK),
-            wg_raw_w[:].bitcast(U16).rearrange("p (b m t) -> p b m t", b=2, t=PACK),
-        )
-        nc.vector.tensor_copy(
-            wg_s[:].rearrange("p (b t m) -> p b m t", b=2, t=PACK),
-            wg_raw_s[:].rearrange("p (b m t) -> p b m t", b=2, t=PACK),
-        )
-        goal = [keep.tile([P, PACK, S], F32, name="goal%d" % b) for b in range(2)]
-        for b in range(2):
-            for t in range(PACK):
-                n = PACK * b + t
-                acc = bank(n, [P, S])
-                nc.tensor.matmul_mx(
-                    out=acc[:],
-                    lhsT=wg_w[:, 2 * P * n : 2 * P * (n + 1)].bitcast(FP4X4),
-                    lhsT_scale=wg_s[:, P * n : P * (n + 1)],
-                    rhs=v_w[:].bitcast(FP8X4),
-                    rhs_scale=v_s[:],
-                    start=True,
-                    stop=True,
-                )
-                nc.scalar.copy(goal[b][:, t, :], acc[:])
 
         x_w = [keep.tile([P, S], U32, name="x_w%d" % a, align_bytes=ALIGN) for a in range(2)]
         x_s = [keep.tile([P, S], U8, name="x_s%d" % a, align_bytes=ALIGN) for a in range(2)]
@@ -236,11 +201,11 @@ def tile_list_replay_goal_value_kernel(
         h_w = [keep.tile([P, S], U32, name="h_w%d" % b, align_bytes=ALIGN) for b in range(2)]
         h_s = [keep.tile([P, S], U8, name="h_s%d" % b, align_bytes=ALIGN) for b in range(2)]
 
-        def add_goal(b, gated, cols, h):
+        def add_goal(gated, goal, h):
             nc.vector.tensor_tensor(
                 h.rearrange("p (c e) t -> p c t e", e=4),
-                gated[:, :, cols].rearrange("p t (c e) -> p c t e", e=4),
-                goal[b][:, :, cols].rearrange("p t (c e) -> p c t e", e=4),
+                gated.rearrange("p t (c e) -> p c t e", e=4),
+                goal.rearrange("p t (c e) -> p c t e", e=4),
                 ADD,
             )
 
@@ -250,6 +215,52 @@ def tile_list_replay_goal_value_kernel(
         b00, b01, a00, a01 = ("b", 0, 0), ("b", 0, 1), ("a", 0, 0), ("a", 0, 1)
         b10, b11, a10, a11 = ("b", 1, 0), ("b", 1, 1), ("a", 1, 0), ("a", 1, 1)
         picks(0, "SS")
+        dealt = bank(2, [P, PACK, P])
+        for t in range(PACK):
+            nc.tensor.transpose(dealt[:, t, :], wgt_rows[:, t:S:PACK], identity[:])
+        nc.scalar.copy(bb_sb[:], dealt[:, :, HEADS : HEADS + 2].rearrange("p t b -> p b t"))
+
+        v_w = keep.tile([P, S], U32, name="v_w", align_bytes=ALIGN)
+        v_s = keep.tile([P, S], U8, name="v_s", align_bytes=ALIGN)
+        nc.vector.tensor_copy(v_w[:], tab_w[:].indirect(goal_list[:]))
+        nc.vector.tensor_copy(v_s[:], tab_s[:].indirect(goal_list[:]))
+        wg_w = keep.tile([P, 2 * H], U8, name="wg_w", align_bytes=ALIGN)
+        wg_s = keep.tile([P, H], U8, name="wg_s", align_bytes=ALIGN)
+        nc.vector.tensor_copy(
+            wg_w[:].bitcast(U16).rearrange("p (b t m) -> p b m t", b=2, t=PACK),
+            wg_raw_w[:].bitcast(U16).rearrange("p (b m t) -> p b m t", b=2, t=PACK),
+        )
+        nc.vector.tensor_copy(
+            wg_s[:].rearrange("p (b t m) -> p b m t", b=2, t=PACK),
+            wg_raw_s[:].rearrange("p (b m t) -> p b m t", b=2, t=PACK),
+        )
+        chunks = [slice(c, c + TAIL) for c in range(0, S, TAIL)]
+
+        def goal_pass(acc, tile, cols):
+            nc.tensor.matmul_mx(
+                out=acc,
+                lhsT=wg_w[:, 2 * P * tile : 2 * P * (tile + 1)].bitcast(FP4X4),
+                lhsT_scale=wg_s[:, P * tile : P * (tile + 1)],
+                rhs=v_w[:, cols].bitcast(FP8X4),
+                rhs_scale=v_s[:, cols],
+                start=True,
+                stop=True,
+            )
+
+        def goal_piece(c, n):
+            acc = bank(n, [P, PACK, TAIL])
+            for t in range(PACK):
+                goal_pass(acc[:, t, :], PACK + t, chunks[c])
+            return acc
+
+        goal0 = keep.tile([P, PACK, S], F32, name="goal0")
+        for t in range(PACK):
+            acc = bank(4 + t, [P, S])
+            goal_pass(acc[:], t, slice(0, S))
+            nc.scalar.copy(goal0[:, t, :], acc[:])
+        goal_last = keep.tile([P, PACK, TAIL], F32, name="goal_last")
+        nc.scalar.copy(goal_last[:], goal_piece(2, 3)[:])
+
         cast(b00, "S", 0, 128)
         picks(1, "SV", lambda: quantize_w(b00))
         logits = banks(0)
@@ -275,8 +286,8 @@ def tile_list_replay_goal_value_kernel(
         quantize_w(b10)
         logits = banks(0)
         project("b", 1, 0, logits)
-        add_goal(0, gated0, slice(0, S // 2), h0[:, : S // 2, :])
-        add_goal(0, gated0, slice(S // 2, S), h0[:, S // 2 :, :])
+        add_goal(gated0[:, :, : S // 2], goal0[:, :, : S // 2], h0[:, : S // 2, :])
+        add_goal(gated0[:, :, S // 2 :], goal0[:, :, S // 2 :], h0[:, S // 2 :, :])
         cast(b11, "S", 0, 128)
         quantize_w(b11)
         project("b", 1, 1, logits)
@@ -293,42 +304,52 @@ def tile_list_replay_goal_value_kernel(
         quantize_w(a11, 2, 4)
         quantize_h(0, h0[:, S // 2 :, :], slice(S // 2, S))
         project("a", 1, 1, feats)
+        goal = {c: goal_piece(c, n) for n, c in enumerate((0, 1, 3))}
         apply_gate(feats, gated1)
 
         out_rows = out.rearrange("(h p) j -> p h j", p=P)
-        chunks = [slice(c, c + TAIL) for c in range(0, S, TAIL)]
 
-        def value_pass(acc, u, b, cols):
+        def value_pass(acc, u, b, cols, start, stop):
             nc.tensor.matmul_mx(
-                out=acc[:],
+                out=acc,
                 lhsT=wv_w[:, b, P * u : P * (u + 1)].bitcast(FP8X4),
                 lhsT_scale=wv_s[:, b, P * u : P * (u + 1)],
                 rhs=h_w[b][:, cols].bitcast(FP8X4),
                 rhs_scale=h_s[b][:, cols],
-                start=(b == 0),
-                stop=(b == 1),
+                start=start,
+                stop=stop,
             )
 
-        values = [[bank(c + 4 * u, [P, TAIL]) for u in range(2)] for c in range(len(chunks))]
-        for u in range(2):
-            for c, cols in enumerate(chunks):
-                value_pass(values[c][u], u, 0, cols)
+        last = len(chunks) - 1
+        values = [bank(4 + c, [P, 2, TAIL]) for c in range(last)]
+        apart = [bank(n, [P, TAIL]) for n in (7, 3)]
         h1 = [halves.tile([P, TAIL, PACK], BF16, name="h1_%d" % c, bufs=1, align_bytes=ALIGN) for c in range(len(chunks))]
-        add_goal(1, gated1, chunks[0], h1[0][:])
-        for c, cols in enumerate(chunks):
-            if c + 1 < len(chunks):
-                add_goal(1, gated1, chunks[c + 1], h1[c + 1][:])
-            quantize_h(1, h1[c][:], cols)
+        for c in range(last):
             for u in range(2):
-                value_pass(values[c][u], u, 1, cols)
-            if c + 1 < len(chunks):
+                value_pass(values[c][:, u, :], u, 0, chunks[c], u == 0, False)
+        for u in range(2):
+            value_pass(apart[u][:], u, 0, chunks[last], True, False)
+        summed = keep.tile([P, PACK, TAIL], F32, name="summed")
+        nc.gpsimd.tensor_tensor(summed[:], gated1[:, :, chunks[2]], goal_last[:], ADD)
+        nc.scalar.copy(h1[2][:].rearrange("p (c e) t -> p c t e", e=4), summed[:].rearrange("p t (c e) -> p c t e", e=4))
+        for c in range(2):
+            add_goal(gated1[:, :, chunks[c]], goal[c][:], h1[c][:])
+        for c, cols in enumerate(chunks):
+            quantize_h(1, h1[c][:], cols)
+            if c == 1:
+                add_goal(gated1[:, :, chunks[last]], goal[last][:], h1[last][:])
+            if c < last:
+                for u in range(2):
+                    value_pass(values[c][:, u, :], u, 1, cols, False, u == 1)
                 result = stage.tile([P, 2, TAIL], F32, name="result", bufs=3)
                 for u in range(2):
-                    nc.scalar.activation(result[:, u, :], values[c][u][:], IDENTITY, bias=bv_sb[:, u : u + 1])
+                    nc.scalar.activation(result[:, u, :], values[c][:, u, :], IDENTITY, bias=bv_sb[:, u : u + 1])
                 nc.sync.dma_start(out_rows[:, :, cols], result[:])
             else:
-                last = [stage.tile([P, TAIL], F32, name="last%d" % u, bufs=1) for u in range(2)]
-                nc.scalar.activation(last[0][:], values[c][0][:], IDENTITY, bias=bv_sb[:, 0:1])
-                nc.vector.tensor_scalar_add(last[1][:], values[c][1][:], bv_sb[:, 1:2])
                 for u in range(2):
-                    nc.sync.dma_start(out_rows[:, u, cols], last[u][:])
+                    value_pass(apart[u][:], u, 1, cols, False, True)
+                final = [stage.tile([P, TAIL], F32, name="last%d" % u, bufs=1) for u in range(2)]
+                nc.scalar.activation(final[0][:], apart[0][:], IDENTITY, bias=bv_sb[:, 0:1])
+                nc.vector.tensor_scalar_add(final[1][:], apart[1][:], bv_sb[:, 1:2])
+                for u in range(2):
+                    nc.sync.dma_start(out_rows[:, u, cols], final[u][:])

@@ -64,9 +64,6 @@ def tile_list_replay_goal_value_kernel(
         nc.gpsimd.memset(wgt_rows[:], 0.0)
         identity = keep.tile([P, P], F32, name="identity")
         make_identity(nc, identity[:])
-        warm = keep.tile([P, 2], F32, name="warm")
-        nc.vector.memset(warm[:, 0:1], 0.0)
-        nc.scalar.activation(warm[:, 1:2], warm[:, 0:1], SIGMOID)
         nc.vector.memset(tab_s[:].bitcast(I32), 0)
         nc.vector.memset(wg_raw_s[:].bitcast(I32), 0)
         nc.vector.memset(wv_s[:].rearrange("p a e -> p (a e)").bitcast(I32), 0)

@@ -148,7 +148,8 @@ def tile_list_replay_goal_value_kernel(
 
         def cast(key, engine, first, last, t0=0, t1=PACK):
             if key not in rounded:
-                rounded[key] = halves.tile([P, PACK, P, PACK], BF16, name="half", align_bytes=ALIGN)
+                own = key == ("a", 1, 1)
+                rounded[key] = halves.tile([P, PACK, P, PACK], BF16, name="a11" if own else "half", bufs=1 if own else 4, align_bytes=ALIGN)
             per_piece = P // len(raw_w[key])
             raw = raw_w[key][first // per_piece]
             at = first % per_piece
@@ -169,7 +170,7 @@ def tile_list_replay_goal_value_kernel(
                 in_=rounded[key][:, first:last].rearrange("p t m j -> p (t m j)"),
             )
 
-        def project(name, b, a, accs, tiles=range(PACK)):
+        def project(name, b, a, accs, tiles=range(PACK), opens=0):
             for t in tiles:
                 cols = slice(P * t, P * (t + 1))
                 nc.tensor.matmul_mx(
@@ -178,8 +179,8 @@ def tile_list_replay_goal_value_kernel(
                     lhsT_scale=w_s[(name, b, a)][:, cols],
                     rhs=x_w[a][:].bitcast(FP8X4),
                     rhs_scale=x_s[a][:],
-                    start=(a == 0),
-                    stop=(a == 1),
+                    start=(a == opens),
+                    stop=(a != opens),
                 )
 
         def banks(first):
@@ -283,25 +284,33 @@ def tile_list_replay_goal_value_kernel(
         quantize_w(b10)
         logits = banks(0)
         project("b", 1, 0, logits)
-        add_goal(gated0[:, :, : S // 2], goal0[:, :, : S // 2], h0[:, : S // 2, :])
-        add_goal(gated0[:, :, S // 2 :], goal0[:, :, S // 2 :], h0[:, S // 2 :, :])
-        cast(b11, "S", 0, 128)
+        cast(b11, "V", 0, 128, 0, 2)
+        cast(b11, "S", 0, 128, 2, 4)
         quantize_w(b11)
         project("b", 1, 1, logits)
         cast(a10, "V", 0, 128, 0, 2)
         cast(a10, "S", 0, 128, 2, 4)
         quantize_w(a10)
         feats = banks(4)
-        project("a", 1, 0, feats)
+        project("a", 1, 0, feats, (0, 1))
         cast(a11, "V", 0, 128, 0, 2)
         cast(a11, "S", 0, 128, 2, 4)
         gated1 = gate(1, logits)
-        quantize_h(0, h0[:, : S // 2, :], slice(0, S // 2))
         quantize_w(a11, 0, 2)
+        add_goal(gated0[:, :, : S // 2], goal0[:, :, : S // 2], h0[:, : S // 2, :])
+        quantize_h(0, h0[:, : S // 2, :], slice(0, S // 2))
         quantize_w(a11, 2, 4)
-        quantize_h(0, h0[:, S // 2 :, :], slice(S // 2, S))
-        project("a", 1, 1, feats)
+        project("a", 1, 1, feats, (0, 1))
+        for t in (2, 3):
+            for a in (1, 0):
+                project("a", 1, a, feats, [t], 1)
         goal = {c: goal_piece(c, n) for n, c in enumerate((0, 1, 3))}
+        summed0 = halves.tile([P, 2, PACK, TAIL], F32, name="a11", bufs=1, align_bytes=ALIGN)
+        for c in (2, 3):
+            nc.gpsimd.tensor_tensor(summed0[:, c - 2], gated0[:, :, chunks[c]], goal0[:, :, chunks[c]], ADD)
+            nc.scalar.copy(
+                h0[:, chunks[c], :].rearrange("p (c e) t -> p c t e", e=4), summed0[:, c - 2].rearrange("p t (c e) -> p c t e", e=4)
+            )
         apply_gate(feats, gated1)
 
         out_rows = out.rearrange("(h p) j -> p h j", p=P)
@@ -321,11 +330,9 @@ def tile_list_replay_goal_value_kernel(
         values = [bank(4 + c, [P, 2, TAIL]) for c in range(last)]
         apart = [bank(n, [P, TAIL]) for n in (7, 3)]
         h1 = [halves.tile([P, TAIL, PACK], BF16, name="h1_%d" % c, bufs=1, align_bytes=ALIGN) for c in range(len(chunks))]
-        for c in range(last):
+        for c in range(2):
             for u in range(2):
                 value_pass(values[c][:, u, :], u, 0, chunks[c], u == 0, False)
-        for u in range(2):
-            value_pass(apart[u][:], u, 0, chunks[last], True, False)
         summed = keep.tile([P, PACK, TAIL], F32, name="summed")
         nc.gpsimd.tensor_tensor(summed[:], gated1[:, :, chunks[2]], goal_last[:], ADD)
         nc.scalar.copy(h1[2][:].rearrange("p (c e) t -> p c t e", e=4), summed[:].rearrange("p t (c e) -> p c t e", e=4))
@@ -334,6 +341,11 @@ def tile_list_replay_goal_value_kernel(
         for c, cols in enumerate(chunks):
             quantize_h(1, h1[c][:], cols)
             if c == 1:
+                quantize_h(0, h0[:, S // 2 :, :], slice(S // 2, S))
+                for u in range(2):
+                    value_pass(values[2][:, u, :], u, 0, chunks[2], u == 0, False)
+                for u in range(2):
+                    value_pass(apart[u][:], u, 0, chunks[last], True, False)
                 add_goal(gated1[:, :, chunks[last]], goal[last][:], h1[last][:])
             if c < last:
                 for u in range(2):

@@ -25,6 +25,7 @@ KP = P * PACK
 ALIGN = 64
 TAIL = 128
 HEADS = 8
+BESIDE = 192
 
 
 def tile_list_replay_goal_value_kernel(
@@ -40,9 +41,9 @@ def tile_list_replay_goal_value_kernel(
 
     with ExitStack() as ctx:
         keep = ctx.enter_context(tc.tile_pool(name="keep", bufs=1))
-        big = ctx.enter_context(tc.tile_pool(name="big", bufs=10))
+        big = ctx.enter_context(tc.tile_pool(name="big", bufs=11))
         stage = ctx.enter_context(tc.tile_pool(name="stage", bufs=2))
-        halves = ctx.enter_context(tc.tile_pool(name="halves", bufs=4))
+        halves = ctx.enter_context(tc.tile_pool(name="halves", bufs=8))
         psum = ctx.enter_context(tc.psum_pool(name="psum", bufs=1))
 
         def bank(n, shape):
@@ -69,16 +70,18 @@ def tile_list_replay_goal_value_kernel(
         nc.vector.memset(wv_s[:].rearrange("p a e -> p (a e)").bitcast(I32), 0)
 
         def load_x(a, i):
-            plane = keep.tile([P, T], F32, name="last_plane", align_bytes=ALIGN) if (a, i) == (1, 3) else big.tile([P, T], F32, name="big")
+            plane = big.tile([P, T], F32, name="big")
             rows = xT[a * KP : (a + 1) * KP, :].rearrange("(p i) t -> p i t", i=PACK)
             nc.sync.dma_start(plane[:], rows[:, i, :])
             return plane
 
-        def load_w(w, b, a, pool, tag, first=0, width=KP):
-            raw = pool.tile([P, PACK, width], F32, name=tag)
-            src = w[a * KP : (a + 1) * KP, b * KP + first : b * KP + first + width]
-            nc.sync.dma_start(raw[:], src.rearrange("(p j) c -> p j c", j=PACK))
+        def load_w(w, b, a, raw):
+            src = w[a * KP : (a + 1) * KP, b * KP : (b + 1) * KP]
+            nc.sync.dma_start(raw, src.rearrange("(p j) c -> p j c", j=PACK))
             return raw
+
+        def ring_slot():
+            return big.tile([P, PACK, KP], F32, name="big")[:]
 
         nc.sync.dma_start(tab_w[:].bitcast(I32), tab_words[0].rearrange("p t i -> p (t i)").bitcast(I32))
         nc.sync.dma_start(wgt_rows[0:HEADS, :], wgt[0 : P : P // HEADS, :])
@@ -94,17 +97,18 @@ def tile_list_replay_goal_value_kernel(
         for r in range(4):
             nc.sync.dma_start(wg_raw_s[r:P:32, :].bitcast(I32), wg_scales[0, r:16:4, :].bitcast(I32))
         raw_w = {}
+        last_rows = keep.tile([P, PACK, KP], F32, name="last_rows")
         for n in range(3, 8):
             if n == 5:
-                raw_w[("b", 0, 0)] = [load_w(wb, 0, 0, big, "big")]
+                raw_w[("b", 0, 1)] = load_w(wb, 0, 1, ring_slot())
             x_planes[(n // 4, n % 4)] = load_x(n // 4, n % 4)
         for b in range(2):
             for name, w in (("b", wb), ("a", wa)):
                 for a in range(2):
-                    if (name, b, a) in (("a", 0, 0), ("a", 1, 1)):
-                        raw_w[(name, b, a)] = [load_w(w, b, a, keep, "gated%d" % b)]
-                    elif (name, b, a) != ("b", 0, 0):
-                        raw_w[(name, b, a)] = [load_w(w, b, a, big, "big")]
+                    if (name, b, a) == ("a", 1, 1):
+                        raw_w[(name, b, a)] = load_w(w, b, a, last_rows[:])
+                    elif (name, b, a) != ("b", 0, 1):
+                        raw_w[(name, b, a)] = load_w(w, b, a, ring_slot())
         nc.sync.dma_start(wv_w[:].bitcast(I32), wv_words.rearrange("a p e i -> p a (e i)").bitcast(I32))
         for r in range(4):
             nc.sync.dma_start(
@@ -126,12 +130,14 @@ def tile_list_replay_goal_value_kernel(
         x_w = [keep.tile([P, S], U32, name="x_w%d" % a, align_bytes=ALIGN) for a in range(2)]
         x_s = [keep.tile([P, S], U8, name="x_s%d" % a, align_bytes=ALIGN) for a in range(2)]
 
-        def picks(a, engines, between=None):
+        def picks(a, engines):
             picked = stage.tile([P, PACK, S], F32, name="picked")
             for i in range(PACK):
-                nc.vector.tensor_tensor(picked[:, i, :], x_planes[(a, i)][:].indirect(head_lists[:]), wgt_sb[:], MULT)
-            if between:
-                between()
+                parts = 2 if (a, i) == (1, PACK - 1) else 1
+                for u in range(parts):
+                    cols = slice(u * S // parts, (u + 1) * S // parts)
+                    offsets = head_lists[:, u * S // parts // 16 : (u + 1) * S // parts // 16]
+                    nc.vector.tensor_tensor(picked[:, i, cols], x_planes[(a, i)][:].indirect(offsets), wgt_sb[:, cols], MULT)
             woven = stage.tile([P, S, PACK], BF16, name="woven", align_bytes=ALIGN)
             for u, engine in enumerate(engines):
                 cols = slice(u * S // 2, (u + 1) * S // 2)
@@ -142,59 +148,53 @@ def tile_list_replay_goal_value_kernel(
                 )
             nc.vector.quantize_mx(out=x_w[a][:].bitcast(FP8X4), scales=x_s[a][:], in_=woven[:].rearrange("p j i -> p (j i)"))
 
-        w_w, w_s = {}, {}
+        w_w, w_s, rounded = {}, {}, {}
+        held_codes = {("b", 1, 0): "gate0"}
 
-        rounded = {}
-
-        def cast(key, engine, first, last, t0=0, t1=PACK):
-            if key not in rounded:
-                own = key == ("a", 1, 1)
-                rounded[key] = halves.tile([P, PACK, P, PACK], BF16, name="a11" if own else "half", bufs=1 if own else 4, align_bytes=ALIGN)
-            per_piece = P // len(raw_w[key])
-            raw = raw_w[key][first // per_piece]
-            at = first % per_piece
+        def cast(key, pair, engine):
+            tile = halves.tile([P, 2, P, PACK], BF16, name="pair", align_bytes=ALIGN)
+            rounded[(key, pair)] = tile
             cast_copy(
                 engine,
-                rounded[key][:, t0:t1].rearrange("p t m j -> p m j t")[:, first:last],
-                raw[:].rearrange("p j (m t) -> p m j t", t=PACK)[:, at : at + last - first, :, t0:t1],
+                tile[:].rearrange("p t m j -> p m j t"),
+                raw_w[key].rearrange("p j (m t) -> p m j t", t=PACK)[:, :, :, 2 * pair : 2 * pair + 2],
             )
 
-        def quantize_w(key, first=0, last=PACK):
+        def quantize_w(key, pair):
             if key not in w_w:
-                w_w[key] = keep.tile([P, KP], U32, name="last_plane" if key == ("b", 0, 0) else "w_w_%s%d%d" % key, align_bytes=ALIGN)
-                w_s[key] = keep.tile([P, KP], U8, name="w_s_%s%d%d" % key, align_bytes=ALIGN)
-            cols = slice(P * first, P * last)
+                label = "%s%d%d" % key
+                w_w[key] = keep.tile([P, KP], U32, name=held_codes.get(key, "w_w_" + label), align_bytes=ALIGN)
+                w_s[key] = keep.tile([P, KP], U8, name="w_s_" + label, align_bytes=ALIGN)
+            cols = slice(2 * P * pair, 2 * P * (pair + 1))
             nc.vector.quantize_mx(
                 out=w_w[key][:, cols].bitcast(FP8X4),
                 scales=w_s[key][:, cols],
-                in_=rounded[key][:, first:last].rearrange("p t m j -> p (t m j)"),
+                in_=rounded[(key, pair)][:].rearrange("p t m j -> p (t m j)"),
             )
 
-        def project(name, b, a, accs, tiles=range(PACK), opens=0):
+        def project(key, accs, tiles, opens):
+            a = key[2]
             for t in tiles:
                 cols = slice(P * t, P * (t + 1))
                 nc.tensor.matmul_mx(
                     out=accs[t][:],
-                    lhsT=w_w[(name, b, a)][:, cols].bitcast(FP8X4),
-                    lhsT_scale=w_s[(name, b, a)][:, cols],
+                    lhsT=w_w[key][:, cols].bitcast(FP8X4),
+                    lhsT_scale=w_s[key][:, cols],
                     rhs=x_w[a][:].bitcast(FP8X4),
                     rhs_scale=x_s[a][:],
-                    start=(a == opens),
-                    stop=(a != opens),
+                    start=opens,
+                    stop=not opens,
                 )
 
         def banks(first):
             return [bank(first + t, [P, S]) for t in range(PACK)]
 
-        def gate(b, logits):
-            gated = keep.tile([P, PACK, S], F32, name="gated%d" % b)
+        def gate(b, logits, gated):
             for t in range(PACK):
                 nc.scalar.activation(gated[:, t, :], logits[t][:], SIGMOID, bias=bb_sb[:, b, t : t + 1])
-            return gated
 
-        def apply_gate(feats, gated):
-            for t in range(PACK):
-                nc.vector.tensor_tensor(gated[:, t, :], feats[t][:], gated[:, t, :], MULT)
+        def apply_gate(feats, gated, t, cols):
+            nc.vector.tensor_tensor(gated[:, t, cols], feats[t][:, cols], gated[:, t, cols], MULT)
 
         h_w = [keep.tile([P, S], U32, name="h_w%d" % b, align_bytes=ALIGN) for b in range(2)]
         h_s = [keep.tile([P, S], U8, name="h_s%d" % b, align_bytes=ALIGN) for b in range(2)]
@@ -245,73 +245,88 @@ def tile_list_replay_goal_value_kernel(
                 stop=True,
             )
 
-        def goal_piece(c, n):
+        def goal_piece(b, c, n):
             acc = bank(n, [P, PACK, TAIL])
             for t in range(PACK):
-                goal_pass(acc[:, t, :], PACK + t, chunks[c])
+                goal_pass(acc[:, t, :], PACK * b + t, chunks[c])
             return acc
 
-        goal0 = keep.tile([P, PACK, S], F32, name="goal0")
-        for t in range(PACK):
-            acc = bank(4 + t, [P, S])
-            goal_pass(acc[:], t, slice(0, S))
-            nc.scalar.copy(goal0[:, t, :], acc[:])
-        goal_last = keep.tile([P, PACK, TAIL], F32, name="goal_last")
-        nc.scalar.copy(goal_last[:], goal_piece(2, 3)[:])
+        def add_goal_beside(gated, goal, h):
+            nc.gpsimd.tensor_tensor(h, gated.rearrange("p t j -> p j t"), goal, ADD)
 
-        cast(b00, "S", 0, 128)
-        picks(1, "SV", lambda: quantize_w(b00))
+        goal_first = keep.tile([P, 2 * TAIL, PACK], F32, name="goal_first")
+        goal_last = keep.tile([P, TAIL, PACK], F32, name="goal_last")
+        for c in (0, 1):
+            nc.scalar.copy(goal_first[:, chunks[c], :], goal_piece(0, c, 4 + c)[:].rearrange("p t j -> p j t"))
+        nc.scalar.copy(goal_last[:], goal_piece(1, 2, 6)[:].rearrange("p t j -> p j t"))
+
+        low, high = (0, 1), (2, 3)
+        for pair in range(2):
+            cast(b01, pair, "S")
+            quantize_w(b01, pair)
+        picks(1, "SV")
         logits = banks(0)
-        project("b", 0, 0, logits)
-        cast(b01, "V", 0, 128, 0, 2)
-        cast(b01, "S", 0, 128, 2, 4)
-        quantize_w(b01)
-        project("b", 0, 1, logits)
-        cast(a00, "V", 0, 128, 0, 2)
-        cast(a00, "S", 0, 128, 2, 4)
-        gated0 = gate(0, logits)
-        quantize_w(a00)
+        project(b01, logits, low, True)
+        cast(b00, 0, "V")
+        cast(b00, 1, "S")
+        for pair in range(2):
+            quantize_w(b00, pair)
+        project(b00, logits, low, False)
+        for t in high:
+            project(b00, logits, [t], True)
+            project(b01, logits, [t], False)
+        gated0 = keep.tile([P, PACK, S], F32, name="gate0", align_bytes=ALIGN)
+        gate(0, logits, gated0)
         feats = banks(4)
-        project("a", 0, 0, feats)
-        cast(a01, "V", 0, 128, 0, 2)
-        cast(a01, "V", 0, 128, 2, 4)
-        quantize_w(a01, 0, 2)
-        quantize_w(a01, 2, 4)
-        project("a", 0, 1, feats)
-        apply_gate(feats, gated0)
-        h0 = halves.tile([P, S, PACK], BF16, name="h0", bufs=1, align_bytes=ALIGN)
-        cast(b10, "S", 0, 128)
-        quantize_w(b10)
-        logits = banks(0)
-        project("b", 1, 0, logits)
-        cast(b11, "V", 0, 128, 0, 2)
-        cast(b11, "S", 0, 128, 2, 4)
-        quantize_w(b11)
-        project("b", 1, 1, logits)
-        cast(a10, "V", 0, 128, 0, 2)
-        cast(a10, "S", 0, 128, 2, 4)
-        quantize_w(a10)
-        feats = banks(4)
-        project("a", 1, 0, feats, (0, 1))
-        cast(a11, "V", 0, 128, 0, 2)
-        cast(a11, "S", 0, 128, 2, 4)
-        gated1 = gate(1, logits)
-        quantize_w(a11, 0, 2)
-        add_goal(gated0[:, :, : S // 2], goal0[:, :, : S // 2], h0[:, : S // 2, :])
-        quantize_h(0, h0[:, : S // 2, :], slice(0, S // 2))
-        quantize_w(a11, 2, 4)
-        project("a", 1, 1, feats, (0, 1))
-        for t in (2, 3):
-            for a in (1, 0):
-                project("a", 1, a, feats, [t], 1)
-        goal = {c: goal_piece(c, n) for n, c in enumerate((0, 1, 3))}
-        summed0 = halves.tile([P, 2, PACK, TAIL], F32, name="a11", bufs=1, align_bytes=ALIGN)
+        for key in (a00, a01):
+            for pair in range(2):
+                cast(key, pair, "V")
+            for pair in range(2):
+                quantize_w(key, pair)
+            project(key, feats, low + high, key == a00)
+        for pair in range(2):
+            cast(b10, pair, "S")
+        for t in range(PACK):
+            apply_gate(feats, gated0, t, slice(0, BESIDE))
+        h0 = keep.tile([P, S, PACK], BF16, name="h0", align_bytes=ALIGN)
+        add_goal_beside(gated0[:, :, :BESIDE], goal_first[:, :BESIDE, :], h0[:, :BESIDE, :])
+        for t in range(PACK - 1):
+            apply_gate(feats, gated0, t, slice(BESIDE, S))
+        goal = {c: goal_piece(0, c, c + 2) for c in (2, 3)}
+        apply_gate(feats, gated0, PACK - 1, slice(BESIDE, S - TAIL))
+        apply_gate(feats, gated0, PACK - 1, chunks[3])
         for c in (2, 3):
-            nc.gpsimd.tensor_tensor(summed0[:, c - 2], gated0[:, :, chunks[c]], goal0[:, :, chunks[c]], ADD)
-            nc.scalar.copy(
-                h0[:, chunks[c], :].rearrange("p (c e) t -> p c t e", e=4), summed0[:, c - 2].rearrange("p t (c e) -> p c t e", e=4)
-            )
-        apply_gate(feats, gated1)
+            add_goal(gated0[:, :, chunks[c]], goal[c][:], h0[:, chunks[c], :])
+        rest = slice(BESIDE, 2 * TAIL)
+        add_goal(gated0[:, :, rest], goal_first[:, rest, :].rearrange("p j t -> p t j"), h0[:, rest, :])
+        logits = banks(0)
+        for pair in range(2):
+            quantize_w(b10, pair)
+            project(b10, logits, (low, high)[pair], True)
+        for pair in range(2):
+            cast(b11, pair, "S")
+            quantize_w(b11, pair)
+            project(b11, logits, (low, high)[pair], False)
+        cast(a10, 0, "V")
+        quantize_w(a10, 0)
+        feats = banks(4)
+        project(a10, feats, low, True)
+        cast(a10, 1, "S")
+        cast(a11, 0, "V")
+        cast(a11, 1, "S")
+        gated1 = last_rows
+        gate(1, logits, gated1)
+        quantize_w(a10, 1)
+        quantize_w(a11, 0)
+        quantize_w(a11, 1)
+        quantize_h(0, h0[:], slice(0, S))
+        project(a11, feats, low, False)
+        for t in high:
+            project(a11, feats, [t], True)
+            project(a10, feats, [t], False)
+        for t in range(PACK):
+            apply_gate(feats, gated1, t, slice(0, S))
+        goal = {c: goal_piece(1, c, 4 + n) for n, c in enumerate((0, 1, 3))}
 
         out_rows = out.rearrange("(h p) j -> p h j", p=P)
 
@@ -327,25 +342,20 @@ def tile_list_replay_goal_value_kernel(
             )
 
         last = len(chunks) - 1
-        values = [bank(4 + c, [P, 2, TAIL]) for c in range(last)]
-        apart = [bank(n, [P, TAIL]) for n in (7, 3)]
+        values = [bank(n, [P, 2, TAIL]) for n in (7, 4, 5)]
+        apart = [bank(n, [P, TAIL]) for n in (2, 3)]
         h1 = [halves.tile([P, TAIL, PACK], BF16, name="h1_%d" % c, bufs=1, align_bytes=ALIGN) for c in range(len(chunks))]
-        for c in range(2):
-            for u in range(2):
-                value_pass(values[c][:, u, :], u, 0, chunks[c], u == 0, False)
-        summed = keep.tile([P, PACK, TAIL], F32, name="summed")
-        nc.gpsimd.tensor_tensor(summed[:], gated1[:, :, chunks[2]], goal_last[:], ADD)
-        nc.scalar.copy(h1[2][:].rearrange("p (c e) t -> p c t e", e=4), summed[:].rearrange("p t (c e) -> p c t e", e=4))
+        add_goal_beside(gated1[:, :, chunks[2]], goal_last[:], h1[2][:])
         for c in range(2):
             add_goal(gated1[:, :, chunks[c]], goal[c][:], h1[c][:])
+        for u in range(2):
+            value_pass(apart[u][:], u, 0, chunks[last], True, False)
+        for c in range(last):
+            for u in range(2):
+                value_pass(values[c][:, u, :], u, 0, chunks[c], u == 0, False)
         for c, cols in enumerate(chunks):
             quantize_h(1, h1[c][:], cols)
             if c == 1:
-                quantize_h(0, h0[:, S // 2 :, :], slice(S // 2, S))
-                for u in range(2):
-                    value_pass(values[2][:, u, :], u, 0, chunks[2], u == 0, False)
-                for u in range(2):
-                    value_pass(apart[u][:], u, 0, chunks[last], True, False)
                 add_goal(gated1[:, :, chunks[last]], goal[last][:], h1[last][:])
             if c < last:
                 for u in range(2):

@@ -43,7 +43,7 @@ def tile_list_replay_goal_value_kernel(
         keep = ctx.enter_context(tc.tile_pool(name="keep", bufs=1))
         big = ctx.enter_context(tc.tile_pool(name="big", bufs=11))
         stage = ctx.enter_context(tc.tile_pool(name="stage", bufs=2))
-        halves = ctx.enter_context(tc.tile_pool(name="halves", bufs=8))
+        halves = ctx.enter_context(tc.tile_pool(name="halves", bufs=6))
         psum = ctx.enter_context(tc.psum_pool(name="psum", bufs=1))
 
         def bank(n, shape):
@@ -97,7 +97,7 @@ def tile_list_replay_goal_value_kernel(
         for r in range(4):
             nc.sync.dma_start(wg_raw_s[r:P:32, :].bitcast(I32), wg_scales[0, r:16:4, :].bitcast(I32))
         raw_w = {}
-        last_rows = keep.tile([P, PACK, KP], F32, name="last_rows")
+        last_rows = keep.tile([P, PACK, KP], F32, name="last_rows", align_bytes=ALIGN)
         for n in range(3, 8):
             if n == 5:
                 raw_w[("b", 0, 1)] = load_w(wb, 0, 1, ring_slot())
@@ -152,13 +152,22 @@ def tile_list_replay_goal_value_kernel(
         held_codes = {("b", 1, 0): "gate0"}
 
         def cast(key, pair, engine):
-            tile = halves.tile([P, 2, P, PACK], BF16, name="pair", align_bytes=ALIGN)
-            rounded[(key, pair)] = tile
+            if (key, pair) == (("a", 1, 1), 1):
+                tile = keep.tile([P, 2, P, PACK], BF16, name="last_pair", align_bytes=ALIGN)
+            else:
+                tile = halves.tile([P, 2, P, PACK], BF16, name="pair", align_bytes=ALIGN)
+            rounded[(key, pair)] = tile[:]
             cast_copy(
                 engine,
-                tile[:].rearrange("p t m j -> p m j t"),
+                rounded[(key, pair)].rearrange("p t m j -> p m j t"),
                 raw_w[key].rearrange("p j (m t) -> p m j t", t=PACK)[:, :, :, 2 * pair : 2 * pair + 2],
             )
+
+        def cast_whole(key):
+            tile = halves.tile([P, PACK, P, PACK], BF16, name="whole", bufs=2, align_bytes=ALIGN)
+            nc.scalar.copy(tile[:].rearrange("p t m j -> p m j t"), raw_w[key].rearrange("p j (m t) -> p m j t", t=PACK))
+            for pair in range(2):
+                rounded[(key, pair)] = tile[:, 2 * pair : 2 * pair + 2]
 
         def quantize_w(key, pair):
             if key not in w_w:
@@ -169,7 +178,7 @@ def tile_list_replay_goal_value_kernel(
             nc.vector.quantize_mx(
                 out=w_w[key][:, cols].bitcast(FP8X4),
                 scales=w_s[key][:, cols],
-                in_=rounded[(key, pair)][:].rearrange("p t m j -> p (t m j)"),
+                in_=rounded[(key, pair)].rearrange("p t m j -> p (t m j)"),
             )
 
         def project(key, accs, tiles, opens):
@@ -193,22 +202,26 @@ def tile_list_replay_goal_value_kernel(
             for t in range(PACK):
                 nc.scalar.activation(gated[:, t, :], logits[t][:], SIGMOID, bias=bb_sb[:, b, t : t + 1])
 
-        def apply_gate(feats, gated, t, cols):
-            nc.vector.tensor_tensor(gated[:, t, cols], feats[t][:, cols], gated[:, t, cols], MULT)
+        def apply_gate(feats, gated, t, cols, gates=None):
+            nc.vector.tensor_tensor(gated[:, t, cols], feats[t][:, cols], (gated if gates is None else gates)[:, t, cols], MULT)
 
-        h_w = [keep.tile([P, S], U32, name="h_w%d" % b, align_bytes=ALIGN) for b in range(2)]
-        h_s = [keep.tile([P, S], U8, name="h_s%d" % b, align_bytes=ALIGN) for b in range(2)]
+        h_w, h_s = {}, {}
 
-        def add_goal(gated, goal, h):
-            nc.vector.tensor_tensor(
+        def add_goal(gated, goal, h, engine=nc.vector):
+            engine.tensor_tensor(
                 h.rearrange("p (c e) t -> p c t e", e=4),
                 gated.rearrange("p t (c e) -> p c t e", e=4),
                 goal.rearrange("p t (c e) -> p c t e", e=4),
                 ADD,
             )
 
-        def quantize_h(b, h, cols):
-            nc.vector.quantize_mx(out=h_w[b][:, cols].bitcast(FP8X4), scales=h_s[b][:, cols], in_=h.rearrange("p j t -> p (j t)"))
+        def quantize_h(b, h, first, count, slot):
+            words = keep.tile([P, count * TAIL], U32, name=slot, align_bytes=ALIGN)
+            scales = keep.tile([P, count * TAIL], U8, name="h_s%d%d" % (b, first), align_bytes=ALIGN)
+            nc.vector.quantize_mx(out=words[:].bitcast(FP8X4), scales=scales[:], in_=h.rearrange("p j t -> p (j t)"))
+            for n in range(count):
+                h_w[(b, first + n)] = words[:, TAIL * n : TAIL * (n + 1)]
+                h_s[(b, first + n)] = scales[:, TAIL * n : TAIL * (n + 1)]
 
         b00, b01, a00, a01 = ("b", 0, 0), ("b", 0, 1), ("a", 0, 0), ("a", 0, 1)
         b10, b11, a10, a11 = ("b", 1, 0), ("b", 1, 1), ("a", 1, 0), ("a", 1, 1)
@@ -251,18 +264,15 @@ def tile_list_replay_goal_value_kernel(
                 goal_pass(acc[:, t, :], PACK * b + t, chunks[c])
             return acc
 
-        def add_goal_beside(gated, goal, h):
-            nc.gpsimd.tensor_tensor(h, gated.rearrange("p t j -> p j t"), goal, ADD)
-
-        goal_first = keep.tile([P, 2 * TAIL, PACK], F32, name="goal_first")
-        goal_last = keep.tile([P, TAIL, PACK], F32, name="goal_last")
+        goal_first = keep.tile([P, PACK, 2 * TAIL], F32, name="goal_first")
+        goal_last = keep.tile([P, PACK, TAIL], F32, name="goal_last")
         for c in (0, 1):
-            nc.scalar.copy(goal_first[:, chunks[c], :], goal_piece(0, c, 4 + c)[:].rearrange("p t j -> p j t"))
-        nc.scalar.copy(goal_last[:], goal_piece(1, 2, 6)[:].rearrange("p t j -> p j t"))
+            nc.scalar.copy(goal_first[:, :, chunks[c]], goal_piece(0, c, 4 + c)[:])
+        nc.scalar.copy(goal_last[:], goal_piece(1, 2, 6)[:])
 
         low, high = (0, 1), (2, 3)
+        cast_whole(b01)
         for pair in range(2):
-            cast(b01, pair, "S")
             quantize_w(b01, pair)
         picks(1, "SV")
         logits = banks(0)
@@ -284,21 +294,21 @@ def tile_list_replay_goal_value_kernel(
             for pair in range(2):
                 quantize_w(key, pair)
             project(key, feats, low + high, key == a00)
-        for pair in range(2):
-            cast(b10, pair, "S")
+        cast_whole(b10)
         for t in range(PACK):
             apply_gate(feats, gated0, t, slice(0, BESIDE))
         h0 = keep.tile([P, S, PACK], BF16, name="h0", align_bytes=ALIGN)
-        add_goal_beside(gated0[:, :, :BESIDE], goal_first[:, :BESIDE, :], h0[:, :BESIDE, :])
+        add_goal(gated0[:, :, :BESIDE], goal_first[:, :, :BESIDE], h0[:, :BESIDE, :], nc.gpsimd)
         for t in range(PACK - 1):
             apply_gate(feats, gated0, t, slice(BESIDE, S))
         goal = {c: goal_piece(0, c, c + 2) for c in (2, 3)}
         apply_gate(feats, gated0, PACK - 1, slice(BESIDE, S - TAIL))
         apply_gate(feats, gated0, PACK - 1, chunks[3])
+        goal1 = {c: goal_piece(1, c, 6 + c) for c in (0, 1)}
         for c in (2, 3):
             add_goal(gated0[:, :, chunks[c]], goal[c][:], h0[:, chunks[c], :])
         rest = slice(BESIDE, 2 * TAIL)
-        add_goal(gated0[:, :, rest], goal_first[:, rest, :].rearrange("p j t -> p t j"), h0[:, rest, :])
+        add_goal(gated0[:, :, rest], goal_first[:, :, rest], h0[:, rest, :])
         logits = banks(0)
         for pair in range(2):
             quantize_w(b10, pair)
@@ -309,64 +319,67 @@ def tile_list_replay_goal_value_kernel(
             project(b11, logits, (low, high)[pair], False)
         cast(a10, 0, "V")
         quantize_w(a10, 0)
-        feats = banks(4)
+        feats = [bank(n, [P, S]) for n in (4, 5, 0, 1)]
         project(a10, feats, low, True)
         cast(a10, 1, "S")
         cast(a11, 0, "V")
         cast(a11, 1, "S")
-        gated1 = last_rows
-        gate(1, logits, gated1)
+        gate(1, logits, last_rows)
         quantize_w(a10, 1)
         quantize_w(a11, 0)
         quantize_w(a11, 1)
-        quantize_h(0, h0[:], slice(0, S))
+        quantize_h(0, h0[:, : S // 2, :], 0, 2, "last_pair")
         project(a11, feats, low, False)
         for t in high:
             project(a11, feats, [t], True)
             project(a10, feats, [t], False)
+        gated1 = big.tile([P, PACK, S], F32, name="big")
         for t in range(PACK):
-            apply_gate(feats, gated1, t, slice(0, S))
-        goal = {c: goal_piece(1, c, 4 + n) for n, c in enumerate((0, 1, 3))}
+            apply_gate(feats, gated1, t, slice(0, S), last_rows)
+        quantize_h(0, h0[:, S // 2 :, :], 2, 2, "last_rows")
+        goal1[3] = goal_piece(1, 3, 4)
 
         out_rows = out.rearrange("(h p) j -> p h j", p=P)
 
-        def value_pass(acc, u, b, cols, start, stop):
+        def value_pass(acc, u, b, c, start, stop):
             nc.tensor.matmul_mx(
                 out=acc,
                 lhsT=wv_w[:, b, P * u : P * (u + 1)].bitcast(FP8X4),
                 lhsT_scale=wv_s[:, b, P * u : P * (u + 1)],
-                rhs=h_w[b][:, cols].bitcast(FP8X4),
-                rhs_scale=h_s[b][:, cols],
+                rhs=h_w[(b, c)].bitcast(FP8X4),
+                rhs_scale=h_s[(b, c)],
                 start=start,
                 stop=stop,
             )
 
         last = len(chunks) - 1
-        values = [bank(n, [P, 2, TAIL]) for n in (7, 4, 5)]
+        values = [bank(n, [P, 2, TAIL]) for n in (5, 0, 1)]
         apart = [bank(n, [P, TAIL]) for n in (2, 3)]
         h1 = [halves.tile([P, TAIL, PACK], BF16, name="h1_%d" % c, bufs=1, align_bytes=ALIGN) for c in range(len(chunks))]
-        add_goal_beside(gated1[:, :, chunks[2]], goal_last[:], h1[2][:])
+        summed = keep.tile([P, PACK, TAIL], F32, name="summed")
+        nc.gpsimd.tensor_tensor(summed[:], gated1[:, :, chunks[2]], goal_last[:], ADD)
+        nc.scalar.copy(h1[2][:].rearrange("p (c e) t -> p c t e", e=4), summed[:].rearrange("p t (c e) -> p c t e", e=4))
         for c in range(2):
-            add_goal(gated1[:, :, chunks[c]], goal[c][:], h1[c][:])
+            add_goal(gated1[:, :, chunks[c]], goal1[c][:], h1[c][:])
         for u in range(2):
-            value_pass(apart[u][:], u, 0, chunks[last], True, False)
+            value_pass(apart[u][:], u, 0, last, True, False)
         for c in range(last):
             for u in range(2):
-                value_pass(values[c][:, u, :], u, 0, chunks[c], u == 0, False)
+                value_pass(values[c][:, u, :], u, 0, c, u == 0, False)
         for c, cols in enumerate(chunks):
-            quantize_h(1, h1[c][:], cols)
+            quantize_h(1, h1[c][:], c, 1, "h_w1%d" % c)
             if c == 1:
-                add_goal(gated1[:, :, chunks[last]], goal[last][:], h1[last][:])
+                add_goal(gated1[:, :, chunks[last]], goal1[last][:], h1[last][:])
             if c < last:
                 for u in range(2):
-                    value_pass(values[c][:, u, :], u, 1, cols, False, u == 1)
+                    value_pass(values[c][:, u, :], u, 1, c, False, u == 1)
                 result = stage.tile([P, 2, TAIL], F32, name="result", bufs=3)
                 for u in range(2):
                     nc.scalar.activation(result[:, u, :], values[c][:, u, :], IDENTITY, bias=bv_sb[:, u : u + 1])
                 nc.sync.dma_start(out_rows[:, :, cols], result[:])
             else:
                 for u in range(2):
-                    value_pass(apart[u][:], u, 1, cols, False, True)
+                    value_pass(apart[u][:], u, 1, c, False, True)
                 final = [stage.tile([P, TAIL], F32, name="last%d" % u, bufs=1) for u in range(2)]
                 nc.scalar.activation(final[0][:], apart[0][:], IDENTITY, bias=bv_sb[:, 0:1])
                 nc.vector.tensor_scalar_add(final[1][:], apart[1][:], bv_sb[:, 1:2])

@@ -25,7 +25,6 @@ KP = P * PACK
 ALIGN = 64
 TAIL = 128
 HEADS = 8
-BESIDE = 192
 
 
 def tile_list_replay_goal_value_kernel(
@@ -58,7 +57,7 @@ def tile_list_replay_goal_value_kernel(
         wv_w = keep.tile([P, 2, N], U32, name="wv_w", align_bytes=ALIGN)
         wv_s = keep.tile([P, 2, N], U8, name="wv_s", align_bytes=ALIGN)
         wgt_sb = keep.tile([P, S], F32, name="wgt_sb")
-        bb_sb = keep.tile([P, 2, PACK], F32, name="bb_sb")
+        bb_sb = keep.tile([P, 2, PACK], F32, name="bb_sb", align_bytes=ALIGN)
         bv_sb = keep.tile([P, 2], F32, name="bv_sb")
 
         wgt_rows = keep.tile([P, S], F32, name="wgt_rows")
@@ -207,8 +206,8 @@ def tile_list_replay_goal_value_kernel(
 
         h_w, h_s = {}, {}
 
-        def add_goal(gated, goal, h, engine=nc.vector):
-            engine.tensor_tensor(
+        def add_goal(gated, goal, h):
+            nc.vector.tensor_tensor(
                 h.rearrange("p (c e) t -> p c t e", e=4),
                 gated.rearrange("p t (c e) -> p c t e", e=4),
                 goal.rearrange("p t (c e) -> p c t e", e=4),
@@ -264,10 +263,14 @@ def tile_list_replay_goal_value_kernel(
                 goal_pass(acc[:, t, :], PACK * b + t, chunks[c])
             return acc
 
-        goal_first = keep.tile([P, PACK, 2 * TAIL], F32, name="goal_first")
+        def weave_h(h, summed):
+            nc.scalar.copy(h.rearrange("p (c e) t -> p c t e", e=4), summed.rearrange("p t (c e) -> p c t e", e=4))
+
+        first, second = slice(0, S // 2), slice(S // 2, S)
+        goal_beside = keep.tile([P, PACK, S // 2], F32, name="goal_beside")
         goal_last = keep.tile([P, PACK, TAIL], F32, name="goal_last")
-        for c in (0, 1):
-            nc.scalar.copy(goal_first[:, :, chunks[c]], goal_piece(0, c, 4 + c)[:])
+        for c in (2, 3):
+            nc.scalar.copy(goal_beside[:, :, chunks[c - 2]], goal_piece(0, c, 2 + c)[:])
         nc.scalar.copy(goal_last[:], goal_piece(1, 2, 6)[:])
 
         low, high = (0, 1), (2, 3)
@@ -296,19 +299,18 @@ def tile_list_replay_goal_value_kernel(
             project(key, feats, low + high, key == a00)
         cast_whole(b10)
         for t in range(PACK):
-            apply_gate(feats, gated0, t, slice(0, BESIDE))
-        h0 = keep.tile([P, S, PACK], BF16, name="h0", align_bytes=ALIGN)
-        add_goal(gated0[:, :, :BESIDE], goal_first[:, :, :BESIDE], h0[:, :BESIDE, :], nc.gpsimd)
+            apply_gate(feats, gated0, t, second)
+        summed0 = keep.tile([P, PACK, S // 2], F32, name="summed0")
+        nc.gpsimd.tensor_tensor(summed0[:], gated0[:, :, second], goal_beside[:], ADD)
         for t in range(PACK - 1):
-            apply_gate(feats, gated0, t, slice(BESIDE, S))
-        goal = {c: goal_piece(0, c, c + 2) for c in (2, 3)}
-        apply_gate(feats, gated0, PACK - 1, slice(BESIDE, S - TAIL))
-        apply_gate(feats, gated0, PACK - 1, chunks[3])
+            apply_gate(feats, gated0, t, first)
+        goal = [goal_piece(0, c, 4 + c) for c in (0, 1)]
+        for c in (0, 1):
+            apply_gate(feats, gated0, PACK - 1, chunks[c])
         goal1 = {c: goal_piece(1, c, 6 + c) for c in (0, 1)}
-        for c in (2, 3):
+        h0 = keep.tile([P, S // 2, PACK], BF16, name="h0", align_bytes=ALIGN)
+        for c in (0, 1):
             add_goal(gated0[:, :, chunks[c]], goal[c][:], h0[:, chunks[c], :])
-        rest = slice(BESIDE, 2 * TAIL)
-        add_goal(gated0[:, :, rest], goal_first[:, :, rest], h0[:, rest, :])
         logits = banks(0)
         for pair in range(2):
             quantize_w(b10, pair)
@@ -328,15 +330,18 @@ def tile_list_replay_goal_value_kernel(
         quantize_w(a10, 1)
         quantize_w(a11, 0)
         quantize_w(a11, 1)
-        quantize_h(0, h0[:, : S // 2, :], 0, 2, "last_pair")
+        quantize_h(0, h0[:], 0, 2, "last_pair")
         project(a11, feats, low, False)
         for t in high:
             project(a11, feats, [t], True)
             project(a10, feats, [t], False)
         gated1 = big.tile([P, PACK, S], F32, name="big")
-        for t in range(PACK):
+        for t in range(PACK - 1):
             apply_gate(feats, gated1, t, slice(0, S), last_rows)
-        quantize_h(0, h0[:, S // 2 :, :], 2, 2, "last_rows")
+        for cols in (first, second):
+            apply_gate(feats, gated1, PACK - 1, cols, last_rows)
+        h0_beside = keep.tile([P, S // 2, PACK], BF16, name="bb_sb", align_bytes=ALIGN)
+        weave_h(h0_beside[:], summed0[:])
         goal1[3] = goal_piece(1, 3, 4)
 
         out_rows = out.rearrange("(h p) j -> p h j", p=P)
@@ -358,17 +363,20 @@ def tile_list_replay_goal_value_kernel(
         h1 = [halves.tile([P, TAIL, PACK], BF16, name="h1_%d" % c, bufs=1, align_bytes=ALIGN) for c in range(len(chunks))]
         summed = keep.tile([P, PACK, TAIL], F32, name="summed")
         nc.gpsimd.tensor_tensor(summed[:], gated1[:, :, chunks[2]], goal_last[:], ADD)
-        nc.scalar.copy(h1[2][:].rearrange("p (c e) t -> p c t e", e=4), summed[:].rearrange("p t (c e) -> p c t e", e=4))
+        weave_h(h1[2][:], summed[:])
         for c in range(2):
             add_goal(gated1[:, :, chunks[c]], goal1[c][:], h1[c][:])
-        for u in range(2):
-            value_pass(apart[u][:], u, 0, last, True, False)
-        for c in range(last):
+        for c in range(2):
             for u in range(2):
                 value_pass(values[c][:, u, :], u, 0, c, u == 0, False)
         for c, cols in enumerate(chunks):
             quantize_h(1, h1[c][:], c, 1, "h_w1%d" % c)
             if c == 1:
+                quantize_h(0, h0_beside[:], 2, 2, "h_w02")
+                for u in range(2):
+                    value_pass(values[2][:, u, :], u, 0, 2, u == 0, False)
+                for u in range(2):
+                    value_pass(apart[u][:], u, 0, last, True, False)
                 add_goal(gated1[:, :, chunks[last]], goal1[last][:], h1[last][:])
             if c < last:
                 for u in range(2):

@@ -96,7 +96,7 @@ def tile_list_replay_goal_value_kernel(
         for r in range(4):
             nc.sync.dma_start(wg_raw_s[r:P:32, :].bitcast(I32), wg_scales[0, r:16:4, :].bitcast(I32))
         raw_w = {}
-        last_rows = keep.tile([P, PACK, KP], F32, name="last_rows", align_bytes=ALIGN)
+        last_rows = keep.tile([P, PACK + 1, KP], F32, name="last_rows", align_bytes=ALIGN)
         for n in range(3, 8):
             if n == 5:
                 raw_w[("b", 0, 1)] = load_w(wb, 0, 1, ring_slot())
@@ -105,7 +105,7 @@ def tile_list_replay_goal_value_kernel(
             for name, w in (("b", wb), ("a", wa)):
                 for a in range(2):
                     if (name, b, a) == ("a", 1, 1):
-                        raw_w[(name, b, a)] = load_w(w, b, a, last_rows[:])
+                        raw_w[(name, b, a)] = load_w(w, b, a, last_rows[:, 1:, :])
                     elif (name, b, a) != ("b", 0, 1):
                         raw_w[(name, b, a)] = load_w(w, b, a, ring_slot())
         nc.sync.dma_start(wv_w[:].bitcast(I32), wv_words.rearrange("a p e i -> p a (e i)").bitcast(I32))
@@ -150,17 +150,20 @@ def tile_list_replay_goal_value_kernel(
         w_w, w_s, rounded = {}, {}, {}
         held_codes = {("b", 1, 0): "gate0"}
 
-        def cast(key, pair, engine):
-            if (key, pair) == (("a", 1, 1), 1):
+        def cast(key, pair, engines):
+            if (key, pair) == (("b", 1, 1), 1):
                 tile = keep.tile([P, 2, P, PACK], BF16, name="last_pair", align_bytes=ALIGN)
             else:
                 tile = halves.tile([P, 2, P, PACK], BF16, name="pair", align_bytes=ALIGN)
             rounded[(key, pair)] = tile[:]
-            cast_copy(
-                engine,
-                rounded[(key, pair)].rearrange("p t m j -> p m j t"),
-                raw_w[key].rearrange("p j (m t) -> p m j t", t=PACK)[:, :, :, 2 * pair : 2 * pair + 2],
-            )
+            each = 2 // len(engines)
+            for n, engine in enumerate(engines):
+                t = 2 * pair + each * n
+                cast_copy(
+                    engine,
+                    tile[:, each * n : each * (n + 1)].rearrange("p t m j -> p m j t"),
+                    raw_w[key].rearrange("p j (m t) -> p m j t", t=PACK)[:, :, :, t : t + each],
+                )
 
         def cast_whole(key):
             tile = halves.tile([P, PACK, P, PACK], BF16, name="whole", bufs=2, align_bytes=ALIGN)
@@ -168,16 +171,16 @@ def tile_list_replay_goal_value_kernel(
             for pair in range(2):
                 rounded[(key, pair)] = tile[:, 2 * pair : 2 * pair + 2]
 
-        def quantize_w(key, pair):
+        def quantize_w(key, pair, first=0, count=2):
             if key not in w_w:
                 label = "%s%d%d" % key
                 w_w[key] = keep.tile([P, KP], U32, name=held_codes.get(key, "w_w_" + label), align_bytes=ALIGN)
                 w_s[key] = keep.tile([P, KP], U8, name="w_s_" + label, align_bytes=ALIGN)
-            cols = slice(2 * P * pair, 2 * P * (pair + 1))
+            cols = slice(P * (2 * pair + first), P * (2 * pair + first + count))
             nc.vector.quantize_mx(
                 out=w_w[key][:, cols].bitcast(FP8X4),
                 scales=w_s[key][:, cols],
-                in_=rounded[(key, pair)].rearrange("p t m j -> p (t m j)"),
+                in_=rounded[(key, pair)][:, first : first + count].rearrange("p t m j -> p (t m j)"),
             )
 
         def project(key, accs, tiles, opens):
@@ -312,14 +315,16 @@ def tile_list_replay_goal_value_kernel(
         for c in (0, 1):
             add_goal(gated0[:, :, chunks[c]], goal[c][:], h0[:, chunks[c], :])
         logits = banks(0)
+        cast(b11, 0, "V")
         for pair in range(2):
             quantize_w(b10, pair)
             project(b10, logits, (low, high)[pair], True)
+        cast(b11, 1, "S")
         for pair in range(2):
-            cast(b11, pair, "S")
             quantize_w(b11, pair)
             project(b11, logits, (low, high)[pair], False)
         cast(a10, 0, "V")
+        quantize_h(0, h0[:], 0, 2, "last_pair")
         quantize_w(a10, 0)
         feats = [bank(n, [P, S]) for n in (4, 5, 0, 1)]
         project(a10, feats, low, True)
@@ -328,9 +333,9 @@ def tile_list_replay_goal_value_kernel(
         cast(a11, 1, "S")
         gate(1, logits, last_rows)
         quantize_w(a10, 1)
-        quantize_w(a11, 0)
+        quantize_w(a11, 0, 0, 1)
+        quantize_w(a11, 0, 1, 1)
         quantize_w(a11, 1)
-        quantize_h(0, h0[:], 0, 2, "last_pair")
         project(a11, feats, low, False)
         for t in high:
             project(a11, feats, [t], True)
@@ -338,7 +343,7 @@ def tile_list_replay_goal_value_kernel(
         gated1 = big.tile([P, PACK, S], F32, name="big")
         for t in range(PACK - 1):
             apply_gate(feats, gated1, t, slice(0, S), last_rows)
-        for cols in (first, second):
+        for cols in (chunks[2], first, chunks[3]):
             apply_gate(feats, gated1, PACK - 1, cols, last_rows)
         h0_beside = keep.tile([P, S // 2, PACK], BF16, name="bb_sb", align_bytes=ALIGN)
         weave_h(h0_beside[:], summed0[:])
@@ -357,39 +362,27 @@ def tile_list_replay_goal_value_kernel(
                 stop=stop,
             )
 
-        last = len(chunks) - 1
-        values = [bank(n, [P, 2, TAIL]) for n in (5, 0, 1)]
-        apart = [bank(n, [P, TAIL]) for n in (2, 3)]
+        values = [[acc[:, u, :] for u in range(2)] for acc in (bank(5, [P, 2, TAIL]), bank(0, [P, 2, TAIL]))]
+        values.extend([[bank(n, [P, TAIL])[:] for n in pair] for pair in ((2, 3), (1, 6))])
         h1 = [halves.tile([P, TAIL, PACK], BF16, name="h1_%d" % c, bufs=1, align_bytes=ALIGN) for c in range(len(chunks))]
         summed = keep.tile([P, PACK, TAIL], F32, name="summed")
         nc.gpsimd.tensor_tensor(summed[:], gated1[:, :, chunks[2]], goal_last[:], ADD)
         weave_h(h1[2][:], summed[:])
         for c in range(2):
             add_goal(gated1[:, :, chunks[c]], goal1[c][:], h1[c][:])
-        for c in range(2):
-            for u in range(2):
-                value_pass(values[c][:, u, :], u, 0, c, u == 0, False)
         for c, cols in enumerate(chunks):
-            quantize_h(1, h1[c][:], c, 1, "h_w1%d" % c)
-            if c == 1:
+            shared = c < 2
+            if c == 2:
                 quantize_h(0, h0_beside[:], 2, 2, "h_w02")
+                add_goal(gated1[:, :, chunks[3]], goal1[3][:], h1[3][:])
+            quantize_h(1, h1[c][:], c, 1, "h_w1%d" % c)
+            for b in range(2):
                 for u in range(2):
-                    value_pass(values[2][:, u, :], u, 0, 2, u == 0, False)
-                for u in range(2):
-                    value_pass(apart[u][:], u, 0, last, True, False)
-                add_goal(gated1[:, :, chunks[last]], goal1[last][:], h1[last][:])
-            if c < last:
-                for u in range(2):
-                    value_pass(values[c][:, u, :], u, 1, c, False, u == 1)
-                result = stage.tile([P, 2, TAIL], F32, name="result", bufs=3)
-                for u in range(2):
-                    nc.scalar.activation(result[:, u, :], values[c][:, u, :], IDENTITY, bias=bv_sb[:, u : u + 1])
-                nc.sync.dma_start(out_rows[:, :, cols], result[:])
+                    value_pass(values[c][u], u, b, c, b == 0 and (u == 0 or not shared), b == 1 and (u == 1 or not shared))
+            result = stage.tile([P, 2, TAIL], F32, name="result", bufs=4)
+            nc.scalar.activation(result[:, 0, :], values[c][0], IDENTITY, bias=bv_sb[:, 0:1])
+            if shared:
+                nc.scalar.activation(result[:, 1, :], values[c][1], IDENTITY, bias=bv_sb[:, 1:2])
             else:
-                for u in range(2):
-                    value_pass(apart[u][:], u, 1, c, False, True)
-                final = [stage.tile([P, TAIL], F32, name="last%d" % u, bufs=1) for u in range(2)]
-                nc.scalar.activation(final[0][:], apart[0][:], IDENTITY, bias=bv_sb[:, 0:1])
-                nc.vector.tensor_scalar_add(final[1][:], apart[1][:], bv_sb[:, 1:2])
-                for u in range(2):
-                    nc.sync.dma_start(out_rows[:, u, cols], final[u][:])
+                nc.vector.tensor_scalar_add(result[:, 1, :], values[c][1], bv_sb[:, 1:2])
+            nc.sync.dma_start(out_rows[:, :, cols], result[:])

@@ -96,7 +96,7 @@ def tile_list_replay_goal_value_kernel(
         for r in range(4):
             nc.sync.dma_start(wg_raw_s[r:P:32, :].bitcast(I32), wg_scales[0, r:16:4, :].bitcast(I32))
         raw_w = {}
-        last_rows = keep.tile([P, PACK + 1, KP], F32, name="last_rows", align_bytes=ALIGN)
+        last_rows = keep.tile([P, PACK, KP], F32, name="last_rows", align_bytes=ALIGN)
         for n in range(3, 8):
             if n == 5:
                 raw_w[("b", 0, 1)] = load_w(wb, 0, 1, ring_slot())
@@ -105,7 +105,7 @@ def tile_list_replay_goal_value_kernel(
             for name, w in (("b", wb), ("a", wa)):
                 for a in range(2):
                     if (name, b, a) == ("a", 1, 1):
-                        raw_w[(name, b, a)] = load_w(w, b, a, last_rows[:, 1:, :])
+                        raw_w[(name, b, a)] = load_w(w, b, a, last_rows[:])
                     elif (name, b, a) != ("b", 0, 1):
                         raw_w[(name, b, a)] = load_w(w, b, a, ring_slot())
         nc.sync.dma_start(wv_w[:].bitcast(I32), wv_words.rearrange("a p e i -> p a (e i)").bitcast(I32))
@@ -156,13 +156,13 @@ def tile_list_replay_goal_value_kernel(
             else:
                 tile = halves.tile([P, 2, P, PACK], BF16, name="pair", align_bytes=ALIGN)
             rounded[(key, pair)] = tile[:]
-            each = 2 // len(engines)
+            each = P // len(engines)
             for n, engine in enumerate(engines):
-                t = 2 * pair + each * n
+                cols = slice(each * n, each * (n + 1))
                 cast_copy(
                     engine,
-                    tile[:, each * n : each * (n + 1)].rearrange("p t m j -> p m j t"),
-                    raw_w[key].rearrange("p j (m t) -> p m j t", t=PACK)[:, :, :, t : t + each],
+                    tile[:].rearrange("p t m j -> p m j t")[:, cols],
+                    raw_w[key].rearrange("p j (m t) -> p m j t", t=PACK)[:, cols, :, 2 * pair : 2 * pair + 2],
                 )
 
         def cast_whole(key):
@@ -297,8 +297,9 @@ def tile_list_replay_goal_value_kernel(
         for key in (a00, a01):
             for pair in range(2):
                 cast(key, pair, "V")
-            for pair in range(2):
-                quantize_w(key, pair)
+            for t in low:
+                quantize_w(key, 0, t, 1)
+            quantize_w(key, 1)
             project(key, feats, low + high, key == a00)
         cast_whole(b10)
         for t in range(PACK):
@@ -310,12 +311,12 @@ def tile_list_replay_goal_value_kernel(
         goal = [goal_piece(0, c, 4 + c) for c in (0, 1)]
         for c in (0, 1):
             apply_gate(feats, gated0, PACK - 1, chunks[c])
-        goal1 = {c: goal_piece(1, c, 6 + c) for c in (0, 1)}
+        goal1 = {0: goal_piece(1, 0, 7)}
         h0 = keep.tile([P, S // 2, PACK], BF16, name="h0", align_bytes=ALIGN)
         for c in (0, 1):
             add_goal(gated0[:, :, chunks[c]], goal[c][:], h0[:, chunks[c], :])
         logits = banks(0)
-        cast(b11, 0, "V")
+        cast(b11, 0, "VS")
         for pair in range(2):
             quantize_w(b10, pair)
             project(b10, logits, (low, high)[pair], True)
@@ -326,7 +327,7 @@ def tile_list_replay_goal_value_kernel(
         cast(a10, 0, "V")
         quantize_h(0, h0[:], 0, 2, "last_pair")
         quantize_w(a10, 0)
-        feats = [bank(n, [P, S]) for n in (4, 5, 0, 1)]
+        feats = [bank(n, [P, S]) for n in (4, 5, 6, 0)]
         project(a10, feats, low, True)
         cast(a10, 1, "S")
         cast(a11, 0, "V")
@@ -347,6 +348,7 @@ def tile_list_replay_goal_value_kernel(
             apply_gate(feats, gated1, PACK - 1, cols, last_rows)
         h0_beside = keep.tile([P, S // 2, PACK], BF16, name="bb_sb", align_bytes=ALIGN)
         weave_h(h0_beside[:], summed0[:])
+        goal1[1] = goal_piece(1, 1, 1)
         goal1[3] = goal_piece(1, 3, 4)
 
         out_rows = out.rearrange("(h p) j -> p h j", p=P)
@@ -362,8 +364,8 @@ def tile_list_replay_goal_value_kernel(
                 stop=stop,
             )
 
-        values = [[acc[:, u, :] for u in range(2)] for acc in (bank(5, [P, 2, TAIL]), bank(0, [P, 2, TAIL]))]
-        values.extend([[bank(n, [P, TAIL])[:] for n in pair] for pair in ((2, 3), (1, 6))])
+        values = [[acc[:, u, :] for u in range(2)] for acc in (bank(5, [P, 2, TAIL]), bank(6, [P, 2, TAIL]))]
+        values.extend([[bank(n, [P, TAIL])[:] for n in pair] for pair in ((2, 3), (0, 7))])
         h1 = [halves.tile([P, TAIL, PACK], BF16, name="h1_%d" % c, bufs=1, align_bytes=ALIGN) for c in range(len(chunks))]
         summed = keep.tile([P, PACK, TAIL], F32, name="summed")
         nc.gpsimd.tensor_tensor(summed[:], gated1[:, :, chunks[2]], goal_last[:], ADD)

@@ -211,9 +211,9 @@ def tile_list_replay_goal_value_kernel(
 
         def add_goal(gated, goal, h):
             nc.vector.tensor_tensor(
-                h.rearrange("p (c e) t -> p c t e", e=4),
-                gated.rearrange("p t (c e) -> p c t e", e=4),
-                goal.rearrange("p t (c e) -> p c t e", e=4),
+                h.rearrange("p (c e) t -> p c t e", e=2),
+                gated.rearrange("p t (c e) -> p c t e", e=2),
+                goal.rearrange("p t (c e) -> p c t e", e=2),
                 ADD,
             )
 

@@ -98,15 +98,13 @@ def tile_list_replay_goal_value_kernel(
         raw_w = {}
         last_rows = keep.tile([P, PACK, KP], F32, name="last_rows", align_bytes=ALIGN)
         for n in range(3, 8):
-            if n == 5:
-                raw_w[("b", 0, 1)] = load_w(wb, 0, 1, ring_slot())
             x_planes[(n // 4, n % 4)] = load_x(n // 4, n % 4)
         for b in range(2):
             for name, w in (("b", wb), ("a", wa)):
                 for a in range(2):
                     if (name, b, a) == ("a", 1, 1):
                         raw_w[(name, b, a)] = load_w(w, b, a, last_rows[:])
-                    elif (name, b, a) != ("b", 0, 1):
+                    else:
                         raw_w[(name, b, a)] = load_w(w, b, a, ring_slot())
         nc.sync.dma_start(wv_w[:].bitcast(I32), wv_words.rearrange("a p e i -> p a (e i)").bitcast(I32))
         for r in range(4):
@@ -277,26 +275,25 @@ def tile_list_replay_goal_value_kernel(
         nc.scalar.copy(goal_last[:], goal_piece(1, 2, 6)[:])
 
         low, high = (0, 1), (2, 3)
-        cast_whole(b01)
-        for pair in range(2):
-            quantize_w(b01, pair)
         picks(1, "SV")
         logits = banks(0)
-        project(b01, logits, low, True)
         cast(b00, 0, "V")
         cast(b00, 1, "S")
         for pair in range(2):
             quantize_w(b00, pair)
-        project(b00, logits, low, False)
-        for t in high:
-            project(b00, logits, [t], True)
-            project(b01, logits, [t], False)
+        project(b00, logits, low + high, True)
+        for pair in range(2):
+            cast(b01, pair, "V")
+        for t in low:
+            quantize_w(b01, 0, t, 1)
+        quantize_w(b01, 1)
+        project(b01, logits, low + high, False)
         gated0 = keep.tile([P, PACK, S], F32, name="gate0", align_bytes=ALIGN)
         gate(0, logits, gated0)
         feats = banks(4)
         for key in (a00, a01):
-            for pair in range(2):
-                cast(key, pair, "V")
+            cast(key, 0, "V")
+            cast(key, 1, "V" if key == a00 else "VS")
             for t in low:
                 quantize_w(key, 0, t, 1)
             quantize_w(key, 1)

@@ -87,18 +87,25 @@ def tile_list_replay_goal_value_kernel(
         nc.sync.dma_start(wgt_rows[HEADS : HEADS + 2, :], bb.rearrange("(b c) -> b c", b=2))
         nc.sync.dma_start(head_lists[:], offs2)
         x_planes = {(0, 0): load_x(0, 0)}
+
+        def load_scales(plane, scales, rows):
+            for r in rows:
+                nc.sync.dma_start(plane[r:P:32, :].bitcast(I32), scales[0, r:16:4, :].bitcast(I32))
+
         nc.sync.dma_start(goal_list[:], offs)
-        for r in range(4):
-            nc.sync.dma_start(tab_s[r:P:32, :].bitcast(I32), tab_scales[0, r:16:4, :].bitcast(I32))
         x_planes[(0, 1)] = load_x(0, 1)
-        nc.sync.dma_start(wg_raw_w[:].bitcast(I32), wg_words[0].bitcast(I32))
+        load_scales(tab_s, tab_scales, (0, 1))
         x_planes[(0, 2)] = load_x(0, 2)
-        for r in range(4):
-            nc.sync.dma_start(wg_raw_s[r:P:32, :].bitcast(I32), wg_scales[0, r:16:4, :].bitcast(I32))
+        load_scales(tab_s, tab_scales, (2, 3))
+        x_planes[(0, 3)] = load_x(0, 3)
+        nc.sync.dma_start(wg_raw_w[:].bitcast(I32), wg_words[0].bitcast(I32))
+        load_scales(wg_raw_s, wg_scales, (0, 1))
+        x_planes[(1, 0)] = load_x(1, 0)
+        load_scales(wg_raw_s, wg_scales, (2, 3))
         raw_w = {}
         last_rows = keep.tile([P, PACK, KP], F32, name="last_rows", align_bytes=ALIGN)
-        for n in range(3, 8):
-            x_planes[(n // 4, n % 4)] = load_x(n // 4, n % 4)
+        for i in range(1, PACK):
+            x_planes[(1, i)] = load_x(1, i)
         for b in range(2):
             for name, w in (("b", wb), ("a", wa)):
                 for a in range(2):

@@ -83,22 +83,22 @@ def tile_list_replay_goal_value_kernel(
             return big.tile([P, PACK, KP], F32, name="big")[:]
 
         nc.sync.dma_start(tab_w[:].bitcast(I32), tab_words[0].rearrange("p t i -> p (t i)").bitcast(I32))
+        nc.sync.dma_start(head_lists[:], offs2)
+        nc.sync.dma_start(goal_list[:], offs)
+        nc.sync.dma_start(wg_raw_w[:].bitcast(I32), wg_words[0].bitcast(I32))
         nc.sync.dma_start(wgt_rows[0:HEADS, :], wgt[0 : P : P // HEADS, :])
         nc.sync.dma_start(wgt_rows[HEADS : HEADS + 2, :], bb.rearrange("(b c) -> b c", b=2))
-        nc.sync.dma_start(head_lists[:], offs2)
         x_planes = {(0, 0): load_x(0, 0)}
 
         def load_scales(plane, scales, rows):
             for r in rows:
                 nc.sync.dma_start(plane[r:P:32, :].bitcast(I32), scales[0, r:16:4, :].bitcast(I32))
 
-        nc.sync.dma_start(goal_list[:], offs)
         x_planes[(0, 1)] = load_x(0, 1)
         load_scales(tab_s, tab_scales, (0, 1))
         x_planes[(0, 2)] = load_x(0, 2)
         load_scales(tab_s, tab_scales, (2, 3))
         x_planes[(0, 3)] = load_x(0, 3)
-        nc.sync.dma_start(wg_raw_w[:].bitcast(I32), wg_words[0].bitcast(I32))
         load_scales(wg_raw_s, wg_scales, (0, 1))
         x_planes[(1, 0)] = load_x(1, 0)
         load_scales(wg_raw_s, wg_scales, (2, 3))

@@ -40,7 +40,7 @@ def tile_list_replay_goal_value_kernel(
 
     with ExitStack() as ctx:
         keep = ctx.enter_context(tc.tile_pool(name="keep", bufs=1))
-        big = ctx.enter_context(tc.tile_pool(name="big", bufs=11))
+        big = ctx.enter_context(tc.tile_pool(name="big", bufs=9))
         stage = ctx.enter_context(tc.tile_pool(name="stage", bufs=2))
         halves = ctx.enter_context(tc.tile_pool(name="halves", bufs=6))
         psum = ctx.enter_context(tc.psum_pool(name="psum", bufs=1))
@@ -103,16 +103,20 @@ def tile_list_replay_goal_value_kernel(
         x_planes[(1, 0)] = load_x(1, 0)
         load_scales(wg_raw_s, wg_scales, (2, 3))
         raw_w = {}
-        last_rows = keep.tile([P, PACK, KP], F32, name="last_rows", align_bytes=ALIGN)
         for i in range(1, PACK):
             x_planes[(1, i)] = load_x(1, i)
+        wb_first = keep.tile([P, PACK, H], F32, name="wb_first")
+        nc.sync.dma_start(wb_first[:], wb[0:KP, :].rearrange("(p j) c -> p j c", j=PACK))
         for b in range(2):
-            for name, w in (("b", wb), ("a", wa)):
-                for a in range(2):
-                    if (name, b, a) == ("a", 1, 1):
-                        raw_w[(name, b, a)] = load_w(w, b, a, last_rows[:])
-                    else:
-                        raw_w[(name, b, a)] = load_w(w, b, a, ring_slot())
+            raw_w[("b", b, 0)] = wb_first[:, :, b * KP : (b + 1) * KP]
+        for name, w, b, a in (("b", wb, 0, 1), ("a", wa, 0, 0), ("a", wa, 0, 1), ("b", wb, 1, 1), ("a", wa, 1, 0)):
+            raw_w[(name, b, a)] = load_w(w, b, a, ring_slot())
+        last_rows = []
+        for u in range(2):
+            rows = keep.tile([P, 2, KP], F32, name="last_rows%d" % u, align_bytes=ALIGN)
+            src = wa[KP : 2 * KP, KP : 2 * KP].rearrange("(p j) c -> p j c", j=PACK)
+            nc.sync.dma_start(rows[:], src[:, 2 * u : 2 * u + 2, :])
+            last_rows.append(rows)
         nc.sync.dma_start(wv_w[:].bitcast(I32), wv_words.rearrange("a p e i -> p a (e i)").bitcast(I32))
         for r in range(4):
             nc.sync.dma_start(
@@ -153,11 +157,13 @@ def tile_list_replay_goal_value_kernel(
             nc.vector.quantize_mx(out=x_w[a][:].bitcast(FP8X4), scales=x_s[a][:], in_=woven[:].rearrange("p j i -> p (j i)"))
 
         w_w, w_s, rounded = {}, {}, {}
-        held_codes = {("b", 1, 0): "gate0"}
+        held_codes = {("b", 1, 1): "gate0", ("b", 1, 0): "first_pair"}
 
         def cast(key, pair, engines):
             if (key, pair) == (("b", 1, 1), 1):
                 tile = keep.tile([P, 2, P, PACK], BF16, name="last_pair", align_bytes=ALIGN)
+            elif (key, pair) == (("b", 0, 1), 1):
+                tile = keep.tile([P, 2, P, PACK], BF16, name="first_pair", align_bytes=ALIGN)
             else:
                 tile = halves.tile([P, 2, P, PACK], BF16, name="pair", align_bytes=ALIGN)
             rounded[(key, pair)] = tile[:]
@@ -175,6 +181,16 @@ def tile_list_replay_goal_value_kernel(
             nc.scalar.copy(tile[:].rearrange("p t m j -> p m j t"), raw_w[key].rearrange("p j (m t) -> p m j t", t=PACK))
             for pair in range(2):
                 rounded[(key, pair)] = tile[:, 2 * pair : 2 * pair + 2]
+
+        def cast_last(u, pair, engine):
+            key = ("a", 1, 1)
+            if (key, pair) not in rounded:
+                rounded[(key, pair)] = halves.tile([P, 2, P, PACK], BF16, name="pair", align_bytes=ALIGN)[:]
+            cast_copy(
+                engine,
+                rounded[(key, pair)].rearrange("p t m j -> p m j t")[:, :, 2 * u : 2 * u + 2, :],
+                last_rows[u][:].rearrange("p j (m t) -> p m j t", t=PACK)[:, :, :, 2 * pair : 2 * pair + 2],
+            )
 
         def quantize_w(key, pair, first=0, count=2):
             if key not in w_w:
@@ -205,12 +221,12 @@ def tile_list_replay_goal_value_kernel(
         def banks(first):
             return [bank(first + t, [P, S]) for t in range(PACK)]
 
-        def gate(b, logits, gated):
+        def gate(b, logits, gates):
             for t in range(PACK):
-                nc.scalar.activation(gated[:, t, :], logits[t][:], SIGMOID, bias=bb_sb[:, b, t : t + 1])
+                nc.scalar.activation(gates[t], logits[t][:], SIGMOID, bias=bb_sb[:, b, t : t + 1])
 
-        def apply_gate(feats, gated, t, cols, gates=None):
-            nc.vector.tensor_tensor(gated[:, t, cols], feats[t][:, cols], (gated if gates is None else gates)[:, t, cols], MULT)
+        def apply_gate(feats, gated, t, cols, gates):
+            nc.vector.tensor_tensor(gated[:, t, cols], feats[t][:, cols], gates[t][:, cols], MULT)
 
         h_w, h_s = {}, {}
 
@@ -284,8 +300,9 @@ def tile_list_replay_goal_value_kernel(
         low, high = (0, 1), (2, 3)
         picks(1, "SV")
         logits = banks(0)
-        cast(b00, 0, "V")
-        cast(b00, 1, "S")
+        for pair in range(2):
+            cast(b00, pair, "V")
+        cast_whole(b10)
         for pair in range(2):
             quantize_w(b00, pair)
         project(b00, logits, low + high, True)
@@ -295,36 +312,36 @@ def tile_list_replay_goal_value_kernel(
             quantize_w(b01, 0, t, 1)
         quantize_w(b01, 1)
         project(b01, logits, low + high, False)
+        for pair in range(2):
+            quantize_w(b10, pair)
         gated0 = keep.tile([P, PACK, S], F32, name="gate0", align_bytes=ALIGN)
-        gate(0, logits, gated0)
+        gates0 = [gated0[:, t, :] for t in range(PACK)]
+        gate(0, logits, gates0)
         feats = banks(4)
         for key in (a00, a01):
             cast(key, 0, "V")
-            cast(key, 1, "V" if key == a00 else "VS")
+            cast(key, 1, "V" if key == a00 else "S")
             for t in low:
                 quantize_w(key, 0, t, 1)
             quantize_w(key, 1)
             project(key, feats, low + high, key == a00)
-        cast_whole(b10)
+        logits = banks(0)
+        project(b10, logits, low + high, True)
+        for pair in range(2):
+            cast(b11, pair, "S")
         for t in range(PACK):
-            apply_gate(feats, gated0, t, second)
+            apply_gate(feats, gated0, t, second, gates0)
         summed0 = keep.tile([P, PACK, S // 2], F32, name="summed0")
         nc.gpsimd.tensor_tensor(summed0[:], gated0[:, :, second], goal_beside[:], ADD)
         for t in range(PACK - 1):
-            apply_gate(feats, gated0, t, first)
+            apply_gate(feats, gated0, t, first, gates0)
         goal = [goal_piece(0, c, 4 + c) for c in (0, 1)]
         for c in (0, 1):
-            apply_gate(feats, gated0, PACK - 1, chunks[c])
+            apply_gate(feats, gated0, PACK - 1, chunks[c], gates0)
         goal1 = {0: goal_piece(1, 0, 7)}
         h0 = keep.tile([P, S // 2, PACK], BF16, name="h0", align_bytes=ALIGN)
         for c in (0, 1):
             add_goal(gated0[:, :, chunks[c]], goal[c][:], h0[:, chunks[c], :])
-        logits = banks(0)
-        cast(b11, 0, "VS")
-        for pair in range(2):
-            quantize_w(b10, pair)
-            project(b10, logits, (low, high)[pair], True)
-        cast(b11, 1, "S")
         for pair in range(2):
             quantize_w(b11, pair)
             project(b11, logits, (low, high)[pair], False)
@@ -334,22 +351,26 @@ def tile_list_replay_goal_value_kernel(
         feats = [bank(n, [P, S]) for n in (4, 5, 6, 0)]
         project(a10, feats, low, True)
         cast(a10, 1, "S")
-        cast(a11, 0, "V")
-        cast(a11, 1, "S")
-        gate(1, logits, last_rows)
+        for pair in range(2):
+            cast_last(0, pair, "S")
+        cast_last(1, 0, "V")
         quantize_w(a10, 1)
         quantize_w(a11, 0, 0, 1)
+        cast_last(1, 1, "V")
         quantize_w(a11, 0, 1, 1)
         quantize_w(a11, 1)
+        gate_pairs = [keep.tile([P, 2, S], F32, name="last_rows%d" % u, align_bytes=ALIGN) for u in range(2)]
+        gates1 = [gate_pairs[t // 2][:, t % 2, :] for t in range(PACK)]
+        gate(1, logits, gates1)
         project(a11, feats, low, False)
         for t in high:
             project(a11, feats, [t], True)
             project(a10, feats, [t], False)
         gated1 = big.tile([P, PACK, S], F32, name="big")
         for t in range(PACK - 1):
-            apply_gate(feats, gated1, t, slice(0, S), last_rows)
+            apply_gate(feats, gated1, t, slice(0, S), gates1)
         for cols in (chunks[2], first, chunks[3]):
-            apply_gate(feats, gated1, PACK - 1, cols, last_rows)
+            apply_gate(feats, gated1, PACK - 1, cols, gates1)
         h0_beside = keep.tile([P, S // 2, PACK], BF16, name="bb_sb", align_bytes=ALIGN)
         weave_h(h0_beside[:], summed0[:])
         goal1[1] = goal_piece(1, 1, 1)

@@ -160,9 +160,7 @@ def tile_list_replay_goal_value_kernel(
         held_codes = {("b", 1, 1): "gate0", ("b", 1, 0): "first_pair"}
 
         def cast(key, pair, engines):
-            if (key, pair) == (("b", 1, 1), 1):
-                tile = keep.tile([P, 2, P, PACK], BF16, name="last_pair", align_bytes=ALIGN)
-            elif (key, pair) == (("b", 0, 1), 1):
+            if (key, pair) == (("b", 0, 1), 1):
                 tile = keep.tile([P, 2, P, PACK], BF16, name="first_pair", align_bytes=ALIGN)
             else:
                 tile = halves.tile([P, 2, P, PACK], BF16, name="pair", align_bytes=ALIGN)
@@ -176,8 +174,8 @@ def tile_list_replay_goal_value_kernel(
                     raw_w[key].rearrange("p j (m t) -> p m j t", t=PACK)[:, cols, :, 2 * pair : 2 * pair + 2],
                 )
 
-        def cast_whole(key):
-            tile = halves.tile([P, PACK, P, PACK], BF16, name="whole", bufs=2, align_bytes=ALIGN)
+        def cast_whole(key, slot):
+            tile = keep.tile([P, PACK, P, PACK], BF16, name=slot, align_bytes=ALIGN)
             nc.scalar.copy(tile[:].rearrange("p t m j -> p m j t"), raw_w[key].rearrange("p j (m t) -> p m j t", t=PACK))
             for pair in range(2):
                 rounded[(key, pair)] = tile[:, 2 * pair : 2 * pair + 2]
@@ -302,7 +300,7 @@ def tile_list_replay_goal_value_kernel(
         logits = banks(0)
         for pair in range(2):
             cast(b00, pair, "V")
-        cast_whole(b10)
+        cast_whole(b10, "whole")
         for pair in range(2):
             quantize_w(b00, pair)
         project(b00, logits, low + high, True)
@@ -327,8 +325,7 @@ def tile_list_replay_goal_value_kernel(
             project(key, feats, low + high, key == a00)
         logits = banks(0)
         project(b10, logits, low + high, True)
-        for pair in range(2):
-            cast(b11, pair, "S")
+        cast_whole(b11, "last_pair")
         for t in range(PACK):
             apply_gate(feats, gated0, t, second, gates0)
         summed0 = keep.tile([P, PACK, S // 2], F32, name="summed0")

from contextlib import ExitStack

import concourse.mybir as mybir
from concourse.masks import make_identity

KX, T, KG, TG, S, H, N = 1024, 2048, 512, 1024, 512, 1024, 256
FLOPS = 2 * S * (2 * KX * H + KG * H + H * N)

F32 = mybir.dt.float32
BF16 = mybir.dt.bfloat16
I32 = mybir.dt.int32
U32 = mybir.dt.uint32
U16 = mybir.dt.uint16
U8 = mybir.dt.uint8
FP8X4 = mybir.dt.float8_e4m3fn_x4
FP4X4 = mybir.dt.float4_e2m1fn_x4
MULT = mybir.AluOpType.mult
ADD = mybir.AluOpType.add
SIGMOID = mybir.ActivationFunctionType.Sigmoid
IDENTITY = mybir.ActivationFunctionType.Identity

P = 128
PACK = 4
KP = P * PACK
ALIGN = 64
TAIL = 128
HEADS = 8


def tile_list_replay_goal_value_kernel(
    tc, xT, wgt, offs2, tab_words, tab_scales, offs, wa, wb, bb, wg_words, wg_scales, wv_words, wv_scales, bv, out
):
    nc = tc.nc

    def cast_copy(engine, dst, src):
        if engine == "S":
            nc.scalar.copy(dst, src)
        else:
            nc.vector.tensor_copy(dst, src)

    with ExitStack() as ctx:
        keep = ctx.enter_context(tc.tile_pool(name="keep", bufs=1))
        big = ctx.enter_context(tc.tile_pool(name="big", bufs=9))
        stage = ctx.enter_context(tc.tile_pool(name="stage", bufs=2))
        halves = ctx.enter_context(tc.tile_pool(name="halves", bufs=6))
        psum = ctx.enter_context(tc.psum_pool(name="psum", bufs=1))

        def bank(n, shape):
            return psum.tile(shape, F32, name="bank%d" % n)

        goal_list = keep.tile([P, S // 16], U16, name="goal_list")
        head_lists = keep.tile([P, S // 16], U16, name="head_lists")
        tab_w = keep.tile([P, TG], U32, name="tab_w", align_bytes=ALIGN)
        tab_s = keep.tile([P, TG], U8, name="tab_s", align_bytes=ALIGN)
        wg_raw_w = keep.tile([P, 2 * H], U8, name="wg_raw_w", align_bytes=ALIGN)
        wg_raw_s = keep.tile([P, H], U8, name="wg_raw_s", align_bytes=ALIGN)
        wv_w = keep.tile([P, 2, N], U32, name="wv_w", align_bytes=ALIGN)
        wv_s = keep.tile([P, 2, N], U8, name="wv_s", align_bytes=ALIGN)
        wgt_sb = keep.tile([P, S], F32, name="wgt_sb")
        bb_sb = keep.tile([P, 2, PACK], F32, name="bb_sb", align_bytes=ALIGN)
        bv_sb = keep.tile([P, 2], F32, name="bv_sb")

        wgt_rows = keep.tile([P, S], F32, name="wgt_rows")
        nc.gpsimd.memset(wgt_rows[:], 0.0)
        identity = keep.tile([P, P], F32, name="identity")
        make_identity(nc, identity[:])
        nc.vector.memset(tab_s[:].bitcast(I32), 0)
        nc.vector.memset(wg_raw_s[:].bitcast(I32), 0)
        nc.vector.memset(wv_s[:].rearrange("p a e -> p (a e)").bitcast(I32), 0)

        def load_x(a, i):
            plane = big.tile([P, T], F32, name="big")
            rows = xT[a * KP : (a + 1) * KP, :].rearrange("(p i) t -> p i t", i=PACK)
            nc.sync.dma_start(plane[:], rows[:, i, :])
            return plane

        def load_w(w, b, a, raw):
            src = w[a * KP : (a + 1) * KP, b * KP : (b + 1) * KP]
            nc.sync.dma_start(raw, src.rearrange("(p j) c -> p j c", j=PACK))
            return raw

        def ring_slot():
            return big.tile([P, PACK, KP], F32, name="big")[:]

        nc.sync.dma_start(tab_w[:].bitcast(I32), tab_words[0].rearrange("p t i -> p (t i)").bitcast(I32))
        nc.sync.dma_start(head_lists[:], offs2)
        nc.sync.dma_start(goal_list[:], offs)
        nc.sync.dma_start(wg_raw_w[:].bitcast(I32), wg_words[0].bitcast(I32))
        nc.sync.dma_start(wgt_rows[0:HEADS, :], wgt[0 : P : P // HEADS, :])
        nc.sync.dma_start(wgt_rows[HEADS : HEADS + 2, :], bb.rearrange("(b c) -> b c", b=2))
        x_planes = {(0, 0): load_x(0, 0)}

        def load_scales(plane, scales, rows):
            for r in rows:
                nc.sync.dma_start(plane[r:P:32, :].bitcast(I32), scales[0, r:16:4, :].bitcast(I32))

        x_planes[(0, 1)] = load_x(0, 1)
        load_scales(tab_s, tab_scales, (0, 1))
        x_planes[(0, 2)] = load_x(0, 2)
        load_scales(tab_s, tab_scales, (2, 3))
        x_planes[(0, 3)] = load_x(0, 3)
        load_scales(wg_raw_s, wg_scales, (0, 1))
        x_planes[(1, 0)] = load_x(1, 0)
        load_scales(wg_raw_s, wg_scales, (2, 3))
        raw_w = {}
        for i in range(1, PACK):
            x_planes[(1, i)] = load_x(1, i)
        wb_first = keep.tile([P, PACK, H], F32, name="wb_first")
        nc.sync.dma_start(wb_first[:], wb[0:KP, :].rearrange("(p j) c -> p j c", j=PACK))
        for b in range(2):
            raw_w[("b", b, 0)] = wb_first[:, :, b * KP : (b + 1) * KP]
        for name, w, b, a in (("b", wb, 0, 1), ("a", wa, 0, 0), ("a", wa, 0, 1), ("b", wb, 1, 1), ("a", wa, 1, 0)):
            raw_w[(name, b, a)] = load_w(w, b, a, ring_slot())
        last_rows = []
        for u in range(2):
            rows = keep.tile([P, 2, KP], F32, name="last_rows%d" % u, align_bytes=ALIGN)
            src = wa[KP : 2 * KP, KP : 2 * KP].rearrange("(p j) c -> p j c", j=PACK)
            nc.sync.dma_start(rows[:], src[:, 2 * u : 2 * u + 2, :])
            last_rows.append(rows)
        nc.sync.dma_start(wv_w[:].bitcast(I32), wv_words.rearrange("a p e i -> p a (e i)").bitcast(I32))
        for r in range(4):
            nc.sync.dma_start(
                wv_s[r:P:32, :, :].bitcast(I32), wv_scales[:, r:16:4, :].rearrange("a q e -> q a e").bitcast(I32)
            )
        with nc.allow_non_contiguous_dma(reason="one bias value for each partition and half"):
            nc.sync.dma_start(bv_sb[:], bv.rearrange("(h p) -> p h", p=P))

        turned = bank(0, [P, S // P, P])
        for c in range(S // P):
            nc.tensor.transpose(turned[:, c, :], wgt_rows[:, P * c : P * (c + 1)], identity[:])
        spread = keep.tile([P, S // P, HEADS, P // HEADS], F32, name="wgt_spread")
        nc.scalar.copy(spread[:], turned[:, :, 0:HEADS].unsqueeze(3).to_broadcast([P, S // P, HEADS, P // HEADS]))
        back = bank(1, [P, S // P, P])
        for c in range(S // P):
            nc.tensor.transpose(back[:, c, :], spread[:, c].rearrange("p g r -> p (g r)"), identity[:])
        nc.scalar.copy(wgt_sb[:], back[:].rearrange("p c j -> p (c j)"))

        x_w = [keep.tile([P, S], U32, name="x_w%d" % a, align_bytes=ALIGN) for a in range(2)]
        x_s = [keep.tile([P, S], U8, name="x_s%d" % a, align_bytes=ALIGN) for a in range(2)]

        def picks(a, engines):
            picked = stage.tile([P, PACK, S], F32, name="picked")
            for i in range(PACK):
                parts = 2 if (a, i) == (1, PACK - 1) else 1
                for u in range(parts):
                    cols = slice(u * S // parts, (u + 1) * S // parts)
                    offsets = head_lists[:, u * S // parts // 16 : (u + 1) * S // parts // 16]
                    nc.vector.tensor_tensor(picked[:, i, cols], x_planes[(a, i)][:].indirect(offsets), wgt_sb[:, cols], MULT)
            woven = stage.tile([P, S, PACK], BF16, name="woven", align_bytes=ALIGN)
            for u, engine in enumerate(engines):
                cols = slice(u * S // 2, (u + 1) * S // 2)
                cast_copy(
                    engine,
                    woven[:, cols, :].rearrange("p (c e) i -> p c i e", e=4),
                    picked[:, :, cols].rearrange("p i (c e) -> p c i e", e=4),
                )
            nc.vector.quantize_mx(out=x_w[a][:].bitcast(FP8X4), scales=x_s[a][:], in_=woven[:].rearrange("p j i -> p (j i)"))

        w_w, w_s, rounded = {}, {}, {}
        held_codes = {("b", 1, 1): "gate0", ("b", 1, 0): "first_pair"}

        def cast(key, pair, engines):
            if (key, pair) == (("b", 0, 1), 1):
                tile = keep.tile([P, 2, P, PACK], BF16, name="first_pair", align_bytes=ALIGN)
            else:
                tile = halves.tile([P, 2, P, PACK], BF16, name="pair", align_bytes=ALIGN)
            rounded[(key, pair)] = tile[:]
            each = P // len(engines)
            for n, engine in enumerate(engines):
                cols = slice(each * n, each * (n + 1))
                cast_copy(
                    engine,
                    tile[:].rearrange("p t m j -> p m j t")[:, cols],
                    raw_w[key].rearrange("p j (m t) -> p m j t", t=PACK)[:, cols, :, 2 * pair : 2 * pair + 2],
                )

        def cast_whole(key, slot):
            tile = keep.tile([P, PACK, P, PACK], BF16, name=slot, align_bytes=ALIGN)
            nc.scalar.copy(tile[:].rearrange("p t m j -> p m j t"), raw_w[key].rearrange("p j (m t) -> p m j t", t=PACK))
            for pair in range(2):
                rounded[(key, pair)] = tile[:, 2 * pair : 2 * pair + 2]

        def cast_last(u, pair, engine):
            key = ("a", 1, 1)
            if (key, pair) not in rounded:
                rounded[(key, pair)] = halves.tile([P, 2, P, PACK], BF16, name="pair", align_bytes=ALIGN)[:]
            cast_copy(
                engine,
                rounded[(key, pair)].rearrange("p t m j -> p m j t")[:, :, 2 * u : 2 * u + 2, :],
                last_rows[u][:].rearrange("p j (m t) -> p m j t", t=PACK)[:, :, :, 2 * pair : 2 * pair + 2],
            )

        def quantize_w(key, pair, first=0, count=2):
            if key not in w_w:
                label = "%s%d%d" % key
                w_w[key] = keep.tile([P, KP], U32, name=held_codes.get(key, "w_w_" + label), align_bytes=ALIGN)
                w_s[key] = keep.tile([P, KP], U8, name="w_s_" + label, align_bytes=ALIGN)
            cols = slice(P * (2 * pair + first), P * (2 * pair + first + count))
            nc.vector.quantize_mx(
                out=w_w[key][:, cols].bitcast(FP8X4),
                scales=w_s[key][:, cols],
                in_=rounded[(key, pair)][:, first : first + count].rearrange("p t m j -> p (t m j)"),
            )

        def project(key, accs, tiles, opens):
            a = key[2]
            for t in tiles:
                cols = slice(P * t, P * (t + 1))
                nc.tensor.matmul_mx(
                    out=accs[t][:],
                    lhsT=w_w[key][:, cols].bitcast(FP8X4),
                    lhsT_scale=w_s[key][:, cols],
                    rhs=x_w[a][:].bitcast(FP8X4),
                    rhs_scale=x_s[a][:],
                    start=opens,
                    stop=not opens,
                )

        def banks(first):
            return [bank(first + t, [P, S]) for t in range(PACK)]

        def gate(b, logits, gates):
            for t in range(PACK):
                nc.scalar.activation(gates[t], logits[t][:], SIGMOID, bias=bb_sb[:, b, t : t + 1])

        def apply_gate(feats, gated, t, cols, gates):
            nc.vector.tensor_tensor(gated[:, t, cols], feats[t][:, cols], gates[t][:, cols], MULT)

        h_w, h_s = {}, {}

        def add_goal(gated, goal, h):
            nc.vector.tensor_tensor(
                h.rearrange("p (c e) t -> p c t e", e=2),
                gated.rearrange("p t (c e) -> p c t e", e=2),
                goal.rearrange("p t (c e) -> p c t e", e=2),
                ADD,
            )

        def quantize_h(b, h, first, count, slot):
            words = keep.tile([P, count * TAIL], U32, name=slot, align_bytes=ALIGN)
            scales = keep.tile([P, count * TAIL], U8, name="h_s%d%d" % (b, first), align_bytes=ALIGN)
            nc.vector.quantize_mx(out=words[:].bitcast(FP8X4), scales=scales[:], in_=h.rearrange("p j t -> p (j t)"))
            for n in range(count):
                h_w[(b, first + n)] = words[:, TAIL * n : TAIL * (n + 1)]
                h_s[(b, first + n)] = scales[:, TAIL * n : TAIL * (n + 1)]

        b00, b01, a00, a01 = ("b", 0, 0), ("b", 0, 1), ("a", 0, 0), ("a", 0, 1)
        b10, b11, a10, a11 = ("b", 1, 0), ("b", 1, 1), ("a", 1, 0), ("a", 1, 1)
        picks(0, "SS")
        dealt = bank(2, [P, PACK, P])
        for t in range(PACK):
            nc.tensor.transpose(dealt[:, t, :], wgt_rows[:, t:S:PACK], identity[:])
        nc.scalar.copy(bb_sb[:], dealt[:, :, HEADS : HEADS + 2].rearrange("p t b -> p b t"))

        v_w = keep.tile([P, S], U32, name="v_w", align_bytes=ALIGN)
        v_s = keep.tile([P, S], U8, name="v_s", align_bytes=ALIGN)
        nc.vector.tensor_copy(v_w[:], tab_w[:].indirect(goal_list[:]))
        nc.vector.tensor_copy(v_s[:], tab_s[:].indirect(goal_list[:]))
        wg_w = keep.tile([P, 2 * H], U8, name="wg_w", align_bytes=ALIGN)
        wg_s = keep.tile([P, H], U8, name="wg_s", align_bytes=ALIGN)
        nc.vector.tensor_copy(
            wg_w[:].bitcast(U16).rearrange("p (b t m) -> p b m t", b=2, t=PACK),
            wg_raw_w[:].bitcast(U16).rearrange("p (b m t) -> p b m t", b=2, t=PACK),
        )
        nc.vector.tensor_copy(
            wg_s[:].rearrange("p (b t m) -> p b m t", b=2, t=PACK),
            wg_raw_s[:].rearrange("p (b m t) -> p b m t", b=2, t=PACK),
        )
        chunks = [slice(c, c + TAIL) for c in range(0, S, TAIL)]

        def goal_pass(acc, tile, cols):
            nc.tensor.matmul_mx(
                out=acc,
                lhsT=wg_w[:, 2 * P * tile : 2 * P * (tile + 1)].bitcast(FP4X4),
                lhsT_scale=wg_s[:, P * tile : P * (tile + 1)],
                rhs=v_w[:, cols].bitcast(FP8X4),
                rhs_scale=v_s[:, cols],
                start=True,
                stop=True,
            )

        def goal_piece(b, c, n):
            acc = bank(n, [P, PACK, TAIL])
            for t in range(PACK):
                goal_pass(acc[:, t, :], PACK * b + t, chunks[c])
            return acc

        def weave_h(h, summed):
            nc.scalar.copy(h.rearrange("p (c e) t -> p c t e", e=4), summed.rearrange("p t (c e) -> p c t e", e=4))

        first, second = slice(0, S // 2), slice(S // 2, S)
        goal_beside = keep.tile([P, PACK, S // 2], F32, name="goal_beside")
        goal_last = keep.tile([P, PACK, TAIL], F32, name="goal_last")
        for c in (2, 3):
            nc.scalar.copy(goal_beside[:, :, chunks[c - 2]], goal_piece(0, c, 2 + c)[:])
        nc.scalar.copy(goal_last[:], goal_piece(1, 2, 6)[:])

        low, high = (0, 1), (2, 3)
        picks(1, "SV")
        logits = banks(0)
        for pair in range(2):
            cast(b00, pair, "V")
        cast_whole(b10, "whole")
        for pair in range(2):
            quantize_w(b00, pair)
        project(b00, logits, low + high, True)
        for pair in range(2):
            cast(b01, pair, "V")
        for t in low:
            quantize_w(b01, 0, t, 1)
        quantize_w(b01, 1)
        project(b01, logits, low + high, False)
        for pair in range(2):
            quantize_w(b10, pair)
        gated0 = keep.tile([P, PACK, S], F32, name="gate0", align_bytes=ALIGN)
        gates0 = [gated0[:, t, :] for t in range(PACK)]
        gate(0, logits, gates0)
        feats = banks(4)
        for key in (a00, a01):
            cast(key, 0, "V")
            cast(key, 1, "V" if key == a00 else "S")
            for t in low:
                quantize_w(key, 0, t, 1)
            quantize_w(key, 1)
            project(key, feats, low + high, key == a00)
        logits = banks(0)
        project(b10, logits, low + high, True)
        cast_whole(b11, "last_pair")
        for t in range(PACK):
            apply_gate(feats, gated0, t, second, gates0)
        summed0 = keep.tile([P, PACK, S // 2], F32, name="summed0")
        nc.gpsimd.tensor_tensor(summed0[:], gated0[:, :, second], goal_beside[:], ADD)
        for t in range(PACK - 1):
            apply_gate(feats, gated0, t, first, gates0)
        goal = [goal_piece(0, c, 4 + c) for c in (0, 1)]
        for c in (0, 1):
            apply_gate(feats, gated0, PACK - 1, chunks[c], gates0)
        goal1 = {0: goal_piece(1, 0, 7)}
        h0 = keep.tile([P, S // 2, PACK], BF16, name="h0", align_bytes=ALIGN)
        for c in (0, 1):
            add_goal(gated0[:, :, chunks[c]], goal[c][:], h0[:, chunks[c], :])
        for pair in range(2):
            quantize_w(b11, pair)
            project(b11, logits, (low, high)[pair], False)
        cast(a10, 0, "V")
        quantize_h(0, h0[:], 0, 2, "last_pair")
        quantize_w(a10, 0)
        feats = [bank(n, [P, S]) for n in (4, 5, 6, 0)]
        project(a10, feats, low, True)
        cast(a10, 1, "S")
        for pair in range(2):
            cast_last(0, pair, "S")
        cast_last(1, 0, "V")
        quantize_w(a10, 1)
        quantize_w(a11, 0, 0, 1)
        cast_last(1, 1, "V")
        quantize_w(a11, 0, 1, 1)
        quantize_w(a11, 1)
        gate_pairs = [keep.tile([P, 2, S], F32, name="last_rows%d" % u, align_bytes=ALIGN) for u in range(2)]
        gates1 = [gate_pairs[t // 2][:, t % 2, :] for t in range(PACK)]
        gate(1, logits, gates1)
        project(a11, feats, low, False)
        for t in high:
            project(a11, feats, [t], True)
            project(a10, feats, [t], False)
        gated1 = big.tile([P, PACK, S], F32, name="big")
        for t in range(PACK - 1):
            apply_gate(feats, gated1, t, slice(0, S), gates1)
        for cols in (chunks[2], first, chunks[3]):
            apply_gate(feats, gated1, PACK - 1, cols, gates1)
        h0_beside = keep.tile([P, S // 2, PACK], BF16, name="bb_sb", align_bytes=ALIGN)
        weave_h(h0_beside[:], summed0[:])
        goal1[1] = goal_piece(1, 1, 1)
        goal1[3] = goal_piece(1, 3, 4)

        out_rows = out.rearrange("(h p) j -> p h j", p=P)

        def value_pass(acc, u, b, c, start, stop):
            nc.tensor.matmul_mx(
                out=acc,
                lhsT=wv_w[:, b, P * u : P * (u + 1)].bitcast(FP8X4),
                lhsT_scale=wv_s[:, b, P * u : P * (u + 1)],
                rhs=h_w[(b, c)].bitcast(FP8X4),
                rhs_scale=h_s[(b, c)],
                start=start,
                stop=stop,
            )

        values = [[acc[:, u, :] for u in range(2)] for acc in (bank(5, [P, 2, TAIL]), bank(6, [P, 2, TAIL]))]
        values.extend([[bank(n, [P, TAIL])[:] for n in pair] for pair in ((2, 3), (0, 7))])
        h1 = [halves.tile([P, TAIL, PACK], BF16, name="h1_%d" % c, bufs=1, align_bytes=ALIGN) for c in range(len(chunks))]
        summed = keep.tile([P, PACK, TAIL], F32, name="summed")
        nc.gpsimd.tensor_tensor(summed[:], gated1[:, :, chunks[2]], goal_last[:], ADD)
        weave_h(h1[2][:], summed[:])
        for c in range(2):
            add_goal(gated1[:, :, chunks[c]], goal1[c][:], h1[c][:])
        for c, cols in enumerate(chunks):
            shared = c < 2
            if c == 2:
                quantize_h(0, h0_beside[:], 2, 2, "h_w02")
                add_goal(gated1[:, :, chunks[3]], goal1[3][:], h1[3][:])
            quantize_h(1, h1[c][:], c, 1, "h_w1%d" % c)
            for b in range(2):
                for u in range(2):
                    value_pass(values[c][u], u, b, c, b == 0 and (u == 0 or not shared), b == 1 and (u == 1 or not shared))
            result = stage.tile([P, 2, TAIL], F32, name="result", bufs=4)
            nc.scalar.activation(result[:, 0, :], values[c][0], IDENTITY, bias=bv_sb[:, 0:1])
            if shared:
                nc.scalar.activation(result[:, 1, :], values[c][1], IDENTITY, bias=bv_sb[:, 1:2])
            else:
                nc.vector.tensor_scalar_add(result[:, 1, :], values[c][1], bv_sb[:, 1:2])
            nc.sync.dma_start(out_rows[:, :, cols], result[:])
